import numpy as np, ml_dtypes
CORES = [40,41,42,43,44,45,46,47]
N = 8
BF = ml_dtypes.bfloat16
def gentries(a):
    return np.ascontiguousarray(a.reshape(8, 16, -1).transpose(0, 2, 1)).reshape(8, -1)
def gtable(e):
    e = np.asarray(e); return np.ascontiguousarray(e.reshape(8, -1, 16).transpose(0, 2, 1)).reshape(128, -1).astype(np.int32)
D, W, H, B, T = 2048, 4096, 3, 2, 1024
M = H * B
TOP = np.arange(16)[:, None]
def counts(rng, n):
    return np.minimum(M + ((96 - M) * rng.random((N, 8, 16, n)) ** rng.choice(np.array([1.0, 2.0, 4.0]), (N, 8, 1, n))).astype(np.int64), 95)
def lists(rng, n):
    return np.ascontiguousarray(np.argsort(rng.random((N, 8, M, n)), axis=-1)[..., :T])
def parts(rng):
    return (counts(rng, D), counts(rng, W), rng.integers(1, 4, (N, 8, 16, H)), lists(rng, D), lists(rng, W), rng.integers(0, 16, (N, 8, M, T)), rng.integers(0, 32, (N, 8, M, T)))
def near(p):
    t = p[:, :, 15:]; a = 32 * p[:, :, :15]; v = a // t; i = np.argmin(a - v * t, axis=2)[:, :, None]
    return np.take_along_axis(v, i, 2)[:, :, 0]
def pack(cd, cw, wt, dl, wl, zo, dr):
    b = lambda a, p: np.ascontiguousarray(a).reshape(N, p, -1).astype(np.float32).astype(BF)
    return {"nd": b(cd, 128), "nw": b(cw, 128), "wt": np.ascontiguousarray(wt).reshape(N, 128, H).astype(np.float32),
            "dl": np.stack([gtable(a.reshape(8, -1)) for a in dl]), "wl": np.stack([gtable(a.reshape(8, -1)) for a in wl]), "zo": b(zo, 8), "dr": b(dr, 8)}
def setup_inputs(rng):
    return pack(*parts(rng))
def setup_inputs_drain(rng):
    cd, cw, wt, dl, wl, zo, dr = parts(rng); s = (N, 8, M, T)
    u = np.argsort(rng.random((8, W)), axis=-1)[:, :T]; q = np.argsort(rng.random((N, 8, D)), axis=-1)[..., :T]; zeta = rng.integers(1, 16, (8, T))
    o = np.argsort(rng.random(s), axis=-1)
    dl = np.take_along_axis(np.broadcast_to(q[:, :, None], s), o, 3); wl = np.take_along_axis(np.broadcast_to(u[None, :, None], s), o, 3); zo = np.take_along_axis(np.broadcast_to(zeta[None, :, None], s), o, 3)
    dr[:, ::2] = 0
    for c, n in ((cd, D), (cw, W)):
        k = rng.integers(0, 4, (N, 4, 1, n))
        c[:, ::2] = np.where(k == 3, M + rng.integers(0, 2, (N, 4, 16, n)), np.where(k == 2, M, np.where(TOP == 0, 95, np.where(k == 0, M, c[:, ::2]))))
    i = dl[:, ::2, M - 1][:, :, None, :]; j = wl[:, ::2, M - 1][:, :, None, :]; z = zo[:, ::2, M - 1][:, :, None, :]
    more = 1 + (M - 1) * (TOP == 0) - M * (TOP == z)
    x = np.take_along_axis(cd[:, ::2], i, 3) + more; y = np.take_along_axis(cw[(np.arange(N) + H - 1) % N][:, ::2], j, 3) + more
    p = np.add.accumulate(x * y * wt[:, ::2, :, H - 1][..., None], axis=2)
    dr[:, ::2, M - 1] = np.where(rng.random((N, 4, T)) < 0.5, near(p), 0)
    return pack(cd, cw, wt, dl, wl, zo, dr)
def setup_inputs_ends(rng):
    cd, cw, wt, dl, wl, zo, dr = parts(rng)
    cd[:, 0] = 95; cw[:, 0] = 95; wt[:, 0] = 3; cd[:, 1] = M; cw[:, 1] = M; wt[:, 1] = 1
    dl[:, 2] = np.arange(T); wl[:, 2] = np.arange(W - T, W); dl[:, 3] = np.arange(D - 1, D - T - 1, -1); wl[:, 3] = np.arange(T - 1, -1, -1)
    dl[:, 4] = dl[:, 4, :1].copy(); wl[:, 4] = wl[:1, 4, :1].copy()
    for a, n in ((dl, D), (wl, W)):
        a[:, 5, :, 0] = (n - 1) * (np.arange(M) % 2); a[:, 5, :, T - 1] = (n - 1) * ((np.arange(M) + 1) % 2)
        a[:, 5, :, 1:T - 1] = 1 + np.argsort(rng.random((N, M, n - 2)), axis=-1)[..., :T - 2]
    zo[:, 1:4] = 15 * rng.integers(0, 2, (N, 3, M, T)); dr[:, 1:5] = 31 * rng.integers(0, 2, (N, 4, M, T))
    return pack(cd, cw, wt, dl, wl, zo, dr)
def setup_inputs_spread(rng):
    cd, cw, wt, dl, wl, zo, dr = parts(rng)
    cd, cw = [np.minimum(M + (np.exp2(7 * rng.random((N, 8, 1, n))) * rng.random((N, 8, 16, n))).astype(np.int64), 95) for n in (D, W)]
    wt = np.where(rng.random((N, 8, 16, H)) < rng.random((N, 8, 1, 1)), 1, wt)
    zo = np.minimum((16 * rng.random((N, 8, M, T)) ** np.exp2(rng.integers(-2, 3, (N, 8, M, 1)))).astype(np.int64), 15)
    dr = np.minimum((32 * rng.random((N, 8, M, T)) ** np.exp2(rng.integers(-2, 3, (N, 8, M, 1)))).astype(np.int64), 31)
    return pack(cd, cw, wt, dl, wl, zo, dr)
def setup_inputs_ties(rng):
    cd, cw, wt, dl, wl, zo, dr = parts(rng)
    zeta = rng.integers(0, 16, (1, 8, 1, 1)); up = (TOP == zeta).astype(np.int64)
    cd = rng.integers(M, 95, (N, 8, 1, D)) + up; cw = rng.integers(M, 95, (N, 8, 1, W)) + up
    wt = np.broadcast_to(rng.integers(1, 4, (N, 8, 1, H)), (N, 8, 16, H)); zo = np.broadcast_to(zeta, (N, 8, M, T))
    return pack(cd, cw, wt, dl, wl, zo, dr)
def setup_inputs_gaps(rng):
    cd, cw, wt, dl, wl, zo, dr = parts(rng); s = (N, 3, T)
    a = np.zeros((N, 3, 16, T), np.int64); b = np.zeros((N, 3, 16, T), np.int64)
    a[:, :, 15] = rng.integers(50, 55, s); b[:, :, 15] = rng.integers(50, 55, s)
    goal = 93 * a[:, :, 15] * b[:, :, 15] + rng.integers(-1, 2, s)
    sa = np.zeros((N, 3, 15, T), np.int64); sb = np.zeros((N, 3, 15, T), np.int64); rest = (goal - 7848) // 3
    for k in range(13):
        left = 13 - k; c = rng.integers(75, 96, s); n = (2 * rest + left * c) // (2 * left * c) if k < 12 else rest // c
        if k == 0: c, n = np.full(s, 95), np.full(s, 91)
        sa[:, :, k] = n; sb[:, :, k] = c; rest = rest - n * c
    rem = 7848 + (goal - 7848) % 3 + 3 * rest
    t = rem % 80; t = np.where(t < 9, t + 80, t)
    sa[:, :, 13] = t; sb[:, :, 13] = 81; sa[:, :, 14] = (rem - 81 * t) // 80; sb[:, :, 14] = 80
    flip = rng.random((N, 3, 1, T)) < 0.5; sa, sb = np.where(flip, sb, sa), np.where(flip, sa, sb)
    od = np.argsort(rng.random((N, 3, 15)), axis=-1); ix = np.broadcast_to(od[..., None], (N, 3, 15, T))
    np.put_along_axis(a, ix, sa, 2); np.put_along_axis(b, ix, sb, 2)
    wv = np.full((N, 3, 16), 3); np.put_along_axis(wv, od[..., 13:], 1, 2); wt[:, :3, :, 0] = wv
    up = (TOP == zo[:, :3, 0][:, :, None, :]).astype(np.int64)
    np.put_along_axis(cd[:, :3], dl[:, :3, 0][:, :, None, :], a - 1 + up, 3); np.put_along_axis(cw[:, :3], wl[:, :3, 0][:, :, None, :], b - 1 + up, 3)
    dr[:, :3, 0] = np.where(rng.random(s) < 0.75, 31, dr[:, :3, 0])
    o = np.argsort(rng.random((N, 2, M, T)), axis=-1)
    dl[:, 3:5] = o; wl[:, 3:5] = o - o % 16 + (5 * o + 3) % 16
    dl[:, 4] = D - 1 - dl[:, 4]; wl[:, 4] = W - 1 - wl[:, 4]
    for c, n in ((dl, D), (wl, W)):
        k = rng.random((N, 2, M, n)) - 2 * (np.arange(n) % 16 == rng.integers(0, 16, (N, 2, M, 1)))
        i = np.argsort(k, axis=-1)[..., :T]
        c[:, 5:7] = np.take_along_axis(i, np.argsort(rng.random(i.shape), axis=-1), 3)
    return pack(cd, cw, wt, dl, wl, zo, dr)
def check_inputs(d):
    bad = []
    for k, lo, hi in (("nd", M, 95), ("nw", M, 95), ("wt", 1, 3), ("dl", 0, D - 1), ("wl", 0, W - 1), ("zo", 0, 15), ("dr", 0, 31)):
        a = np.asarray(d[k]).astype(np.float64)
        if not (np.min(a) >= lo and np.max(a) <= hi): bad.append("range of " + k)
        if np.any(a != np.floor(a)): bad.append("whole numbers in " + k)
    for k in ("dl", "wl"):
        s = np.sort(np.stack([gentries(a) for a in d[k]]).reshape(N, 8, M, T), axis=-1)
        if np.any(s[..., 1:] == s[..., :-1]): bad.append("different numbers in a batch of " + k)
    return bad
def reference(nd, nw, wt, dl, wl, zo, dr):
    whole = lambda a: a.astype(np.float32).astype(np.int64)
    docs = whole(nd).reshape(N, 8, 16, D); blocks = whole(nw).reshape(N, 8, 16, W); weight = whole(wt).reshape(N, 8, 16, H)
    dls = np.stack([gentries(a) for a in dl]).astype(np.int64).reshape(N, 8, M, T); wls = np.stack([gentries(a) for a in wl]).astype(np.int64).reshape(N, 8, M, T)
    olds = whole(zo).reshape(N, 8, M, T); draws = whole(dr).reshape(N, 8, M, T); news = np.zeros((N, 8, M, T), np.int64)
    for h in range(H):
        who = (np.arange(N) + h) % N; mine = blocks[who]
        for b in range(B):
            m = h * B + b; di = dls[:, :, m][:, :, None, :]; wi = wls[:, :, m][:, :, None, :]
            old = (olds[:, :, m][:, :, None, :] == TOP).astype(np.int64)
            x = np.take_along_axis(docs, di, 3) - old; y = np.take_along_axis(mine, wi, 3) - old
            p = np.add.accumulate((x + 1) * (y + 1) * weight[:, :, :, h][..., None], axis=2)
            z = np.add.reduce((32 * p <= draws[:, :, m][:, :, None, :] * p[:, :, 15:]).astype(np.int64), axis=2)
            new = (z[:, :, None, :] == TOP).astype(np.int64)
            np.put_along_axis(docs, di, x + new, 3); np.put_along_axis(mine, wi, y + new, 3)
            news[:, :, m] = z
        blocks[who] = mine
    last = blocks[(np.arange(N) + H - 1) % N]
    return {"yd": docs.reshape(N, 128, D).astype(np.float32).astype(BF), "yw": last.reshape(N, 128, W).astype(np.float32).astype(BF), "yz": news.reshape(N, 8, M * T).astype(np.float32).astype(BF)}

@@ -1,0 +1,333 @@
+from concourse.mybir import AluOpType as ALU, ActivationFunctionType as AF
+
+D, W, H, TK, M = 2048, 4096, 3, 1024, 6
+C = 256
+OFF = 135.0
+MAGIC = 12582912.0
+
+SCRATCH = {}
+for _n, _c in (("W0", W), ("W1", W), ("W2", W), ("ndb", D), ("ydb", D), ("zt", M * TK), ("vt", M * TK), ("om", M * TK), ("zr", M * TK),
+               ("sg", 2 * TK), ("ag", TK), ("y1", TK), ("nm", TK), ("nsend", 2 * TK), ("nrecv", 2 * TK), ("zs", 512), ("zw", 112),
+               ("ones", 128), ("sel", 128), ("j1", 128), ("jm", 128), ("tri", 128), ("eye", 128), ("up", 128), ("lx", 128), ("sm", 128),
+               ("t1", 128), ("t2", 128), ("t3", 128), ("icb", 8)):
+    SCRATCH[_n] = ("sbuf", [128, _c], "bfloat16")
+for _n, _c in (("doc", D), ("wts", 4), ("wp", TK), ("wv", TK), ("na", TK), ("triw", 384), ("onew", 384), ("cols", 16)):
+    SCRATCH[_n] = ("sbuf", [128, _c], "float32")
+for _n, _c, _t in (("dli", 384, "int32"), ("wli", 384, "int32"), ("pi", 4, "int32"), ("pj", 4, "int32"),
+                   ("dlu", 384, "uint16"), ("wlu", 384, "uint16"), ("nbo", 192, "uint16")):
+    SCRATCH[_n] = ("sbuf", [128, _c], _t)
+BANKS = ("A0", "A1", "A2", "A3", "D0", "D1", "ZB", "ZZ")
+for _n in BANKS:
+    SCRATCH[_n] = ("psum", [128, 512], "float32")
+DMAS = ["zo", "dl0", "wl0", "dr0", "wt", "nd", "nw", "dr1", "dl1", "wl1", "zr", "yw", "yd0", "yd1", "yz"]
+ARRS = ["off", "blk1", "blk2"] + ["val%d_%d" % (s, k) for s in (0, 1) for k in range(4)]
+SEMAPHORES = ["cv", "cs", "ct", "cg", "sent"] + ["d_" + n for n in DMAS] + ["a_" + n for n in ARRS]
+
+NORM = {"s": "gx0 gx1 gx23 sg0 sg1 cpN0 sg2 cpN1 sa0 cpN2 sg3 sa1 cpN3 cpA3 sa23",
+        "v": "gy0 w0 gy1 wv0 w1 gy2 w2 wv1 gy3 wv2 w3 wv3 vpA0 sb0 vpA1 sb1 vpA2 sb2 sb3",
+        "t": "Xa0 Xa1 Xa2 Xa3 Dw0 Dv0 Dw1 Dw2 Dv1 NB0 Dv2 NB1 Dw3 NB2 Dv3 Np3 NA3 NB3 Z0 pV0 pV1 pV2 Z1 pV3"}
+EDGE = {"s": "gx0 gx1 gx23 sg0 sg1 cpN0 cpN1 sg2 sg3 cpN2 cpN3 sa01 sa23",
+        "v": "gy0 gy1 w0 w1 wv0 wv1 gy2 gy3 w2 w3 wv2 nb0 wv3 nb1 omA vpA0 omB nb2 vpA1 nb3 vpA2 vpA3 rs0 rs1 rs2 rs3",
+        "t": "Xa0 Xa1 Dw0 Dw1 Dv0 Xa2 Xa3 Dv1 NB0 Dw2 NB1 Dw3 Dv2 Dv3 NB2 NB3 pV0 Z0 Z1 pV1 pV2 pV3",
+        "g": "sd0 sd1 sd2 sd3"}
+PLAN = {
+    "npre": 4, "ch": [0, 256, 512, 768, 1024], "nd": 3,
+    "start": {
+        "y": "Lzo Lnd Lnw Lwl1 Ldl1 Ldr1 Lzr",
+        "s": "Ldl0 Ldr0 Lwl0 Lwt",
+        "g": "pi sel j1 jm eye tri up",
+        "v": "ones pj zw0 icol icb e15 ne zc j9 t2 lx t2b om0 id0 iw0 t1 om1 triw0 onew0 t3 zw1 sm om2 om3 triw1 onew1 triw2 onew2",
+        "t": "zb0 zb1 V0 V1 XO0 XO1 V2 V3 zb2 XO2 XO3 zb3",
+    },
+    0: {"s": "gx01 gx23 conv sg0 cpN0 sg1 sa0 cpN1 sg2 sg3 cpN2 sa1 cpN3 cpA3 sa23",
+        "v": "gy0 w0 gy1 wv0 w1 gy2 wv1 gy3 w2 w3 iw1 vpA0 wv2 wv3 sb0 vpA1 sb1 vpA2 sb2 id1 sb3",
+        "t": "Xa0 Xa1 Xa2 Xa3 Dw0 Dv0 Dw1 NB0 Dv1 Dw2 Dw3 NB1 Dv2 Dv3 NB2 Np3 NA3 NB3 pV0 Z0 pV1 pV2 Z1 pV3",
+        "g": "off blk"},
+    1: EDGE,
+    2: dict(NORM, g="blk"),
+    3: EDGE,
+    4: NORM,
+    5: {"s": "gx0 gx1 gx23 sg0 cpN0 sg1 sg2 cpN1 cpN2 sg3 sa0 cpN3 zcp Syz cpA3 sa1 sa23",
+        "v": "gy0 gy1 w0 wv0 w1 gy2 wv1 gy3 w2 w3 wv2 wv3 vpA0 sb0 sb1 vpA1 sb2 sb3 vpA2 fin0 fin1",
+        "t": "Xa0 Xa1 Dw0 Dv0 Xa2 Xa3 Dw1 NB0 Dw2 Dv1 Dv2 NB1 Dw3 NB2 Dv3 Np3 Z0 NA3 NB3 Z1",
+        "y": "Syw Syd0 Syd1"},
+}
+
+
+def build(T, topo, core, g, plan):
+    n = len(T.cores)
+    r = T.rank_of(core)
+    dst = T.cores[(r - 1) % n]
+    rid, pid = topo.addr(dst)[0], topo.addr(dst)[1]
+    mask = topo.mask(core, dst)
+    neng = len(topo.engines(core, dst))
+    nin = len(topo.engines(T.cores[(r + 1) % n], core))
+    V, S, P = g.vector, g.scalar, g.tensor
+    queues = {"y": [], "s": [], "g": [], "v": [], "t": [], "x": []}
+    full = lambda b: (b, 0, 1 << 20)
+
+    def add(q, name, fn, R, Wr, needs, gives=None, kind="c"):
+        R = [full(x) if isinstance(x, str) else x for x in R]
+        Wr = [full(x) if isinstance(x, str) else x for x in Wr]
+        queues[q].append({"q": q, "name": name, "fn": fn, "R": R, "W": Wr, "gives": gives or [name], "needs": needs, "kind": kind})
+
+    def dma(q, name, pairs, R, Wr, needs=()):
+        eng = g.sync if q == "y" else g.scalar
+        add(q, name, lambda: [eng.dma_start(o, i) for o, i in pairs], R, Wr, list(needs), kind="d")
+
+    def remote(name, out, in_, R, Wr, needs):
+        add("g", name, lambda: g.remote_dma(out, in_, T.sem["a_" + name], T.sem.sent, pid, rid, mask), R, [], needs, ["s_" + name], "r")
+        add("x", name, None, [], Wr, [], ["a_" + name], "a")
+
+    def asel(name, rows, pat, op, base, cm, src):
+        add("g", name, lambda: g.affine_select(T[name][0:rows, :], T[src][0:rows, :], pat, op, 0.0, base, cm), [src], [name], [src])
+
+    def ts(name, out, in0, s1, s2, ops, R, Wr, needs, gives=None):
+        add("v", name, lambda: V.tensor_scalar(out, in0, s1, s2, *ops), R, Wr, needs, gives)
+
+    def tt(name, out, in0, in1, op, R, Wr, needs, gives=None):
+        add("v", name, lambda: V.tensor_tensor(out, in0, in1, op), R, Wr, needs, gives)
+
+    def cp(name, out, in_, R, Wr, needs, gives=None):
+        add("v", name, lambda: V.tensor_copy(out, in_), R, Wr, needs, gives)
+
+    def mm(name, out, lhsT, rhs, start, stop, R, Wr, needs, gives=None):
+        add("t", name, lambda: P.matmul(out, lhsT, rhs, start, stop), R, Wr, needs, gives)
+
+    def act(name, out, in_, f, bias, R, Wr, needs, gives=None):
+        if bias: add("s", name, lambda: S.activation(out, in_, f, bias=bias), R, Wr, needs, gives)
+        else: add("s", name, lambda: S.activation(out, in_, f), R, Wr, needs, gives)
+
+    col = lambda k: T.cols[:, 4 * k:4 * k + 1]
+    cr = lambda k: ("cols", k, k + 1)
+    npre, CH, ND = plan["npre"], plan["ch"], plan["nd"]
+    NC = len(CH) - 1
+    ab = lambda m, c: "A%d" % ((m * NC + c) % 4)
+    db = lambda m, c: ("D0", "D1", "ZB")[(m * NC + c) % ND]
+    back = lambda m, c, k: divmod(m * NC + c - k, NC)
+    zb_bank = lambda k: ("D0", "D1", "ZB")[k % 3]
+    last = lambda kk, m=M - 1: ["%s%d_%d" % (kk, m, c) for c in range(NC)]
+    oms = lambda a, b: ["om%d" % (a // 512), "om%d" % ((b - 1) // 512)]
+
+    def pre(m, c, which):
+        A = ab(m, c); k = CH[c + 1] - CH[c]; t0 = m * TK + CH[c]
+        prev = ["cpA%d_%d" % back(m, c, 4), "cpN%d_%d" % back(m, c, 4)] if m * NC + c >= 4 else []
+        if prev and back(m, c, 4)[0] in (1, 3): prev.append("nb%d_%d" % back(m, c, 4))
+        if "V" in which:
+            mm("V%d_%d" % (m, c), T[A][:, C:C + k], T.sel[0:8, :], T.vt[0:8, t0:t0 + k], True, True,
+               ["sel", ("vt", t0, t0 + k)], [A], ["sel", "dr0" if m == 0 else "dr1"] + prev)
+        if "X" in which:
+            mm("XO%d_%d" % (m, c), T[A][:, 0:k], T.lx[:, :], T.om[:, t0:t0 + k], True, False,
+               ["lx", ("om", t0, t0 + k)], [A], ["V%d_%d" % (m, c), "lx"] + oms(t0, t0 + k))
+
+    def fixed(q, w, m):
+        if w == "Lzo": dma(q, "zo", [(T.zt[0:8, 0:npre * 512], T.zo[:, 0:npre * 512])], [], ["zt"])
+        elif w == "Lzr": dma(q, "zr", [(T.zr[i:128:16, npre * 512:], T.zo[:, npre * 512:]) for i in range(16)], [], ["zr"])
+        elif w == "Ldr0": dma(q, "dr0", [(T.vt[0:8, 0:TK], T.dr[:, 0:TK])], [], [("vt", 0, TK)])
+        elif w == "Ldr1": dma(q, "dr1", [(T.vt[0:8, TK:], T.dr[:, TK:])], [], [("vt", TK, M * TK)])
+        elif w[:3] in ("Ldl", "Lwl"):
+            a, b = ((0, 64), (64, 384))[int(w[3])]
+            dma(q, w[1:], [(T[w[1:3] + "i"][:, a:b], T[w[1:3]][:, a:b])], [], [(w[1:3] + "i", a, b)])
+        elif w[:2] in ("id", "iw"):
+            a, b = ((0, 64), (64, 384))[int(w[2])]
+            k = w[1] + "l"
+            cp(w, T[k + "u"][:, a:b], T[k + "i"][:, a:b], [(k + "i", a, b)], [(k + "u", a, b)], [k + w[2]])
+        elif w == "Lwt": dma(q, "wt", [(T.wts[:, 0:3], T.wt[:, :])], [], ["wts"])
+        elif w == "Lnd": dma(q, "nd", [(T.ndb[:, :], T.nd[:, :])], [], ["ndb"])
+        elif w == "Lnw": dma(q, "nw", [(T.W0[:, :], T.nw[:, :])], [], ["W0"])
+        elif w == "pi": add(q, w, lambda: g.iota(T.pi[:, 0:1], [[0, 1]], 0, 1), [], [w], [])
+        elif w == "sel": asel(w, 8, [[1, 8], [0, 16]], ALU.is_equal, 0, -1, "ones")
+        elif w == "j1": asel(w, 128, [[-16, 8], [0, 16]], ALU.is_ge, 0, 1, "ones")
+        elif w == "jm": asel(w, 128, [[16, 8], [0, 16]], ALU.is_ge, 15, -1, "j1")
+        elif w == "tri": asel(w, 128, [[1, 128]], ALU.is_ge, 0, -1, "j1")
+        elif w == "eye": asel(w, 128, [[1, 128]], ALU.is_equal, 0, -1, "ones")
+        elif w == "up": asel(w, 128, [[1, 128]], ALU.is_equal, -1, -1, "j1")
+        elif w == "ones": add(q, w, lambda: V.memset(T.ones[:, :], 1.0), [], [w], [])
+        elif w == "zw0": add(q, w, lambda: V.memset(T.zw[:, :], 0.0), [], ["zw"], [])
+        elif w == "pj": ts(w, T.pj[:, 0:1], T.pi[:, 0:1], 15, None, [ALU.bitwise_and], ["pi"], [w], ["pi"])
+        elif w == "icol": cp(w, col(0), T.pj[:, 0:1], ["pj"], [cr(0)], ["pj"])
+        elif w == "icb": cp(w, T.icb[:, 0:1], col(0), [cr(0)], [w], ["icol"])
+        elif w == "e15": ts(w, col(1), col(0), 15.0, None, [ALU.is_equal], [cr(0)], [cr(1)], ["icol"])
+        elif w == "ne": ts(w, col(2), col(1), -1.0, None, [ALU.mult], [cr(1)], [cr(2)], ["e15"])
+        elif w == "zc": ts(w, col(3), col(1), 8.0, -0.5, [ALU.mult, ALU.add], [cr(1)], [cr(3)], ["e15"])
+        elif w == "j9": ts(w, T.t3[:, :], T.jm[:, :], -9.0, None, [ALU.mult], ["jm"], ["t3"], ["jm"])
+        elif w == "lx": tt(w, T.lx[:, :], T.t3[:, :], T.eye[:, :], ALU.add, ["t3", "eye"], [w], ["j9", "eye"])
+        elif w == "t1": tt(w, T.t1[:, :], T.eye[:, :], T.up[:, :], ALU.subtract, ["up", "eye"], [w], ["up", "eye"])
+        elif w == "t2": ts(w, T.t2[:, :], T.jm[:, :], col(2), None, [ALU.mult], ["jm", cr(2)], [w], ["jm", "ne"])
+        elif w == "t2b": ts(w, T.t2[:, 0:128:16], T.t2[:, 0:128:16], 0.5, None, [ALU.mult], ["t2"], ["t2"], ["t2"])
+        elif w == "t3": ts(w, T.t1[:, :], T.t1[:, :], 0.5, None, [ALU.mult], ["t1"], ["t1"], ["t1"])
+        elif w == "sm": tt(w, T.sm[:, :], T.t1[:, :], T.t2[:, :], ALU.add, ["t1", "t2"], [w], ["t3", "t2b"])
+        elif w == "zw1": ts(w, T.zw[:, 11:96:12], T.jm[:, 0:128:16], col(3), None, [ALU.mult], ["jm", "zw", cr(3)], ["zw"], ["jm", "zc", "zw0"])
+        elif w[:4] in ("triw", "onew"):
+            h = int(w[4]); src, k = ("tri", 32.0) if w[0] == "t" else ("jm", -1.0)
+            ts(w, T[w[:4]][:, h * 128:(h + 1) * 128], T[src][:, :], T.wts[:, h:h + 1], k, [ALU.mult, ALU.mult], [src, "wts"], [(w[:4], h, h + 1)], [src, "wt"])
+        elif w[:2] == "zb":
+            k = int(w[2:]); b = zb_bank(k)
+            mm(w, T[b][:, 0:512], T.sel[0:8, :], T.zt[0:8, k * 512:(k + 1) * 512], True, True, ["sel", "zt"], [b], ["sel", "zo"] + (["om%d" % (k - 3)] if k >= 3 else []))
+        elif w in ("omA", "omB"):
+            k = 2 * (m + 1 + "AB".index(w[2])); a = k * 512
+            ts(w, T.om[:, a:a + TK], T.zr[:, a:a + TK], T.icb[:, 0:1], None, [ALU.not_equal], ["zr", "icb"], [("om", a, a + TK)], ["zr", "icb"], oms(a, a + TK))
+        elif w[:2] == "om":
+            k = int(w[2:]); b = zb_bank(k)
+            ts(w, T.om[:, k * 512:(k + 1) * 512], T[b][:, 0:512], col(0), None, [ALU.not_equal], [b, cr(0)], [("om", k * 512, (k + 1) * 512)], ["zb%d" % k, "icol"])
+        elif w[:2] == "XO": pre(0, int(w[2]), "X")
+        elif w[0] == "V": pre(0, int(w[1]), "V")
+        elif w == "conv": act(w, T.doc[:, :], T.ndb[:, :], AF.Silu, 0, ["ndb"], ["doc"], ["nd"])
+        elif w == "off": remote(w, T.nbo[:, :], T.wlu[:, 64:256], [("wlu", 64, 256)], ["nbo"], ["iw1"])
+        elif w == "blk":
+            a, b = "W%d" % (m // 2), "W%d" % (m // 2 + 1)
+            remote("blk" + b[1], T[b][:, :], T[a][:, :], [a], [b], last("sb", m))
+        elif w == "Syw": dma(q, "yw", [(T.yw[:, :], T.W2[:, :])], ["W2"], [], last("sb"))
+        elif w[:3] == "fin":
+            a = int(w[3]) * TK
+            ts(w, T.ydb[:, a:a + TK], T.doc[:, a:a + TK], MAGIC, MAGIC, [ALU.add, ALU.subtract], ["doc"], [("ydb", a, a + TK)], last("sa"))
+        elif w[:3] == "Syd":
+            a = int(w[3]) * TK
+            dma(q, w[1:], [(T.yd[:, a:a + TK], T.ydb[:, a:a + TK])], [("ydb", a, a + TK)], [], ["fin" + w[3]])
+        elif w == "zcp": act(w, T.zs[0:96, :], T.ZZ[0:96, 0:512], AF.Identity, 0, ["ZZ"], ["zs"], ["Z5_1"])
+        elif w == "Syz": dma(q, "yz", [(T.yz[:, :], T.zs[0:96, :])], ["zs"], [], ["zcp"])
+        else: return False
+        return True
+
+    def chunk(m, w):
+        h = m // 2
+        k = w.rstrip("0123456789")
+        cs = [int(x) for x in w[len(k):]]
+        tag = lambda kk, cc=None, mb=m: ["%s%d_%d" % (kk, mb, c) for c in (cs if cc is None else cc)]
+        c0 = cs[0]; a, b = CH[c0], CH[cs[-1] + 1]; u = min(b - a, C)
+        t0, t1 = m * TK + a, m * TK + b
+        o0, o1 = t0 // 16, t1 // 16
+        e0, e1 = h * TK + a, h * TK + b
+        s0, s1 = (m % 2) * TK + a, (m % 2) * TK + b
+        A = ab(m, c0); Dk = db(m, c0); Wk = "W%d" % h
+        lo, hi, dd = T[A][:, 0:u], T[A][:, C:C + u], T[Dk][:, 0:u]
+        name = "%s_%d" % (w, m)
+        me = tag(k)
+        byact = ("cpA%d" % c0) in plan[m]["s"].split()
+        wordw = lambda: T[Wk][:, 0:W].indirect(T.wlu[:, o0:o1])
+        if k == "gx":
+            src, prev = ("ndb", ["nd", "id0"]) if m == 0 else ("doc", last("sa", m - 1) + ["id1"])
+            act(name, T.ag[:, a:b], T[src][:, 0:D].indirect(T.dlu[:, o0:o1]), AF.Identity, OFF, [src, ("dlu", o0, o1)], [("ag", a, b)], prev, me)
+        elif k == "gy":
+            prev = ["nw", "iw0"] if m == 0 else last("sb", m - 1) + ["iw1"]
+            tt(name, T.y1[:, a:b], wordw(), T.om[:, t0:t1], ALU.add, [Wk, ("wlu", o0, o1), ("om", t0, t1)], [("y1", a, b)], prev + oms(t0, t1), me)
+        elif k == "Xa": mm(name, lo, T.eye[:, :], T.ag[:, a:b], False, True, ["eye", ("ag", a, b)], [A], tag("XO") + tag("gx"), me)
+        elif k == "w": tt(name, T.wp[:, a:b], lo, T.y1[:, a:b], ALU.mult, [A, ("y1", a, b)], [("wp", a, b)], tag("Xa") + tag("gy"), me)
+        elif k == "wv": tt(name, T.wv[:, a:b], hi, T.wp[:, a:b], ALU.mult, [A, ("wp", a, b)], [("wv", a, b)], tag("w"), me)
+        elif k == "Dw":
+            if m * NC + c0 >= ND: prev = ["sg%d_%d" % back(m, c0, ND)]
+            else: prev = ["om%d" % j for j in range(npre) if zb_bank(j) == Dk]
+            mm(name, dd, T.triw[:, h * 128:(h + 1) * 128], T.wp[:, a:b], True, False,
+               [("triw", h, h + 1), ("wp", a, b)], [Dk], tag("w") + prev + ["triw%d" % h], me)
+        elif k == "Dv":
+            mm(name, dd, T.onew[:, h * 128:(h + 1) * 128], T.wv[:, a:b], False, True,
+               [("onew", h, h + 1), ("wv", a, b)], [Dk], tag("Dw") + tag("wv") + ["onew%d" % h], me)
+        elif k == "sg": act(name, T.sg[:, s0:s1], dd, AF.Sign, -0.5, [Dk], [("sg", s0, s1)], tag("Dv") + (["Z%d_1" % (m - 2)] if m >= 2 else []), me)
+        elif k == "Np":
+            mm(name, lo, T.eye[:, :], T.om[:, t0:t1], True, False, ["eye", ("om", t0, t1)], [A], tag("wv"))
+            mm(name + "a", lo, T.eye[:, :], T.ag[:, a:b], False, False, ["eye", ("ag", a, b)], [A], [], me)
+        elif k == "NA": mm(name, lo, T.sm[:, :], T.sg[:, s0:s1], False, True, ["sm", ("sg", s0, s1)], [A], tag("sg") + tag("Np") + ["sm"], me)
+        elif k == "NB": mm(name, hi, T.sm[:, :], T.sg[:, s0:s1], True, True, ["sm", ("sg", s0, s1)], [A], tag("NA" if byact else "sg") + ["sm"], me)
+        elif k == "cpA": act(name, T.na[:, a:b], lo, AF.Identity, -OFF, [A], [("na", a, b)], tag("NB"), me)
+        elif k == "cpN": act(name, T.nm[:, a:b], hi, AF.Identity, 0, [A], [("nm", a, b)], tag("NB"), me)
+        elif k == "vpA": tt(name, T.na[:, a:b], lo, T.nm[:, a:b], ALU.add, [A, ("nm", a, b)], [("na", a, b)], tag("cpN"), tag("cpA"))
+        elif k == "nb":
+            tt(name, T.nsend[:, e0:e1], hi, T.y1[:, a:b], ALU.add, [A, ("y1", a, b)], [("nsend", e0, e1)], tag("NB"),
+               me + ([] if ("cpN%d" % c0) in plan[m]["s"].split() else tag("cpN")))
+        elif k == "sa":
+            act(name, T.doc[:, 0:D].indirect(T.dlu[:, o0:o1]), T.na[:, a:b], AF.Silu, 0, [("na", a, b), ("dlu", o0, o1)], ["doc"],
+                tag("cpA") + last("gx", m) + ["conv"], me)
+        elif k == "sb":
+            tt(name, wordw(), T.y1[:, a:b], T.nm[:, a:b], ALU.add, [("y1", a, b), ("nm", a, b), ("wlu", o0, o1)], [Wk], tag("cpN") + last("gy", m), me)
+        elif k == "sd": remote("val%d_%d" % (h, c0), T.nrecv[:, e0:e1], T.nsend[:, e0:e1], [("nsend", e0, e1)], [("nrecv", e0, e1)], tag("nb"))
+        elif k == "rs":
+            Wn = "W%d" % (h + 1)
+            cp(name, T[Wn][:, 0:W].indirect(T.nbo[:, o0 - 64:o1 - 64]), T.nrecv[:, e0:e1], [("nrecv", e0, e1), "nbo"], [Wn], [], tag("sb"))
+        elif k == "Z":
+            j = 2 * m + c0
+            z0 = (m % 2) * TK + c0 * 512
+            mm(name, T.ZZ[0:96, 0:512], T.zw[:, 11 - j:107 - j], T.sg[:, z0:z0 + 512], j == 0, j == 11, ["zw", ("sg", z0, z0 + 512)], ["ZZ"],
+               tag("sg", [c for c in range(NC) if CH[c] < c0 * 512 + 512 and CH[c + 1] > c0 * 512]) + ["zw1"] + (["Z%d_%d" % divmod(j - 1, 2)] if j else []), me)
+        elif k == "pV":
+            if m + 1 < M: pre(m + 1, c0, "VX")
+        else: raise ValueError(w)
+
+    for m in ["start"] + list(range(M)):
+        for q in "ysvtg":
+            for w in plan[m].get(q, "").split():
+                if not fixed(q, w, m): chunk(m, w)
+
+    order, have, pos = [], set(), {q: 0 for q in queues}
+    moved = True
+    while moved:
+        moved = False
+        for q in "xysgvt":
+            while pos[q] < len(queues[q]) and all(x in have for x in queues[q][pos[q]]["needs"]):
+                o = queues[q][pos[q]]; order.append(o); have.update(o["gives"]); pos[q] += 1; moved = True
+    stuck = [(q, queues[q][pos[q]]["name"], [x for x in queues[q][pos[q]]["needs"] if x not in have]) for q in queues if pos[q] < len(queues[q])]
+    if stuck:
+        raise ValueError("order: %r" % (stuck,))
+    return order, neng, nin
+
+
+def emit(order, neng, nin, g, T):
+    eng = {"y": g.sync, "s": g.scalar, "g": g, "v": g.vector, "t": g.tensor}
+    count = {k: 0 for k in "vstg"}
+    known = {q: {} for q in eng}
+    hist, ends, sent = {}, {}, 0
+    for o in order:
+        q = o["q"]
+        deps = []
+        for write, regs in ((False, o["R"]), (True, o["W"])):
+            for (b, lo, hi) in regs:
+                for e in hist.get(b, []):
+                    if b in BANKS:
+                        if e[3]["q"] != q: deps.append(e[3])
+                    elif e[0] < hi and lo < e[1] and (write or e[2]):
+                        deps.append(e[3])
+        if o["kind"] != "a":
+            kn = known[q]
+            need = {}
+            for d in deps:
+                s, v = d["sig"]
+                if kn.get(s, 0) < v: need[s] = max(need.get(s, 0), v)
+            for d in deps:
+                for s, v in d["clock"].items():
+                    if s != d["sig"][0] and s in need and need[s] <= v:
+                        del need[s]
+            for s in sorted(need):
+                eng[q].wait_ge(T.sem[s], need[s])
+            for d in deps:
+                for s, v in d["clock"].items():
+                    if kn.get(s, 0) < v: kn[s] = v
+            ins = o["fn"]()
+            if o["kind"] == "c":
+                count[q] += 1
+                ins.then_inc(T.sem["c" + q], 1)
+                o["sig"] = ("c" + q, count[q])
+            elif o["kind"] == "d":
+                for i in ins:
+                    i.then_inc(T.sem["d_" + o["name"]], 16)
+                o["sig"] = ("d_" + o["name"], 16 * len(ins))
+            else:
+                sent += neng
+                o["sig"] = ("sent", sent)
+            o["clock"] = dict(kn)
+        else:
+            o["sig"] = ("a_" + o["name"], nin)
+            o["clock"] = {}
+        o["clock"][o["sig"][0]] = o["sig"][1]
+        ends[o["sig"][0]] = o["sig"][1]
+        for (b, lo, hi) in o["W"]:
+            hist[b] = [e for e in hist.get(b, []) if not (lo <= e[0] and e[1] <= hi)] + [(lo, hi, True, o)]
+        for (b, lo, hi) in o["R"]:
+            hist.setdefault(b, []).append((lo, hi, False, o))
+    for s in sorted(ends):
+        g.sync.wait_ge(T.sem[s], ends[s])
+
+
+def rank_program(g, core, T, topo):
+    if T.rank_of(core) is None:
+        return
+    order, neng, nin = build(T, topo, core, g, PLAN)
+    emit(order, neng, nin, g, T)

@@ -1,56 +1,65 @@
 from concourse.mybir import AluOpType as ALU, ActivationFunctionType as AF
 
 D, W, H, TK, M = 2048, 4096, 3, 1024, 6
-C = 256
+B = 128
+PAD = 16
 OFF = 135.0
 MAGIC = 12582912.0
 
 SCRATCH = {}
-for _n, _c in (("W0", W), ("W1", W), ("W2", W), ("ndb", D), ("ydb", D), ("zt", M * TK), ("vt", M * TK), ("om", M * TK), ("zr", M * TK),
-               ("sg", 2 * TK), ("ag", TK), ("y1", TK), ("nm", TK), ("nsend", 2 * TK), ("nrecv", 2 * TK), ("zs", 512), ("zw", 112),
-               ("ones", 128), ("sel", 128), ("j1", 128), ("jm", 128), ("tri", 128), ("eye", 128), ("up", 128), ("lx", 128), ("sm", 128),
-               ("t1", 128), ("t2", 128), ("t3", 128), ("icb", 8)):
+for _n, _c in (("W0", W), ("W1", W), ("W2", W), ("ndb", D), ("ydb", D), ("zt", M * TK), ("om", M * TK), ("zr", M * TK),
+               ("y1", M * TK), ("nm", M * TK), ("yrecv", 2 * TK), ("nrecv", 2 * TK), ("ag", TK), ("vp", 2 * TK),
+               ("ee", TK), ("cv", TK + 8 * PAD), ("cs", TK + 8 * PAD), ("zs", 512), ("zw", 112), ("vt", 384), ("vT", 384), ("pw", 400),
+               ("ones", 384), ("sel", B), ("j1", B), ("jm", B), ("eye", B), ("up", B), ("lx", B), ("hp", B), ("hn", B),
+               ("r0", B), ("t3", B), ("icb", 8)):
     SCRATCH[_n] = ("sbuf", [128, _c], "bfloat16")
-for _n, _c in (("doc", D), ("wts", 4), ("wp", TK), ("wv", TK), ("na", TK), ("triw", 384), ("onew", 384), ("cols", 16)):
+for _n, _c in (("doc", D), ("wts", 4), ("wp", TK), ("na", TK), ("rw", 384), ("cols", 16)):
     SCRATCH[_n] = ("sbuf", [128, _c], "float32")
 for _n, _c, _t in (("dli", 384, "int32"), ("wli", 384, "int32"), ("pi", 4, "int32"), ("pj", 4, "int32"),
-                   ("dlu", 384, "uint16"), ("wlu", 384, "uint16"), ("nbo", 192, "uint16")):
+                   ("dlu", 384, "uint16"), ("wlu", 384, "uint16"), ("nbo", 128, "uint16")):
     SCRATCH[_n] = ("sbuf", [128, _c], _t)
-BANKS = ("A0", "A1", "A2", "A3", "D0", "D1", "ZB", "ZZ")
+BANKS = ("X0", "X1", "X2", "X3", "D0", "D1", "D2", "ZZ")
 for _n in BANKS:
     SCRATCH[_n] = ("psum", [128, 512], "float32")
-DMAS = ["zo", "dl0", "wl0", "dr0", "wt", "nd", "nw", "dr1", "dl1", "wl1", "zr", "yw", "yd0", "yd1", "yz"]
-ARRS = ["off", "blk1", "blk2"] + ["val%d_%d" % (s, k) for s in (0, 1) for k in range(4)]
+DMAS = ["zo", "dl0", "wl0", "dr", "wt", "nd", "nw", "dl1", "wl1", "zr", "yw", "yd0", "yd1", "yz"]
+ARRS = ["off0", "off1", "blk1", "blk2"] + ["%s%d_%d" % (k, s, c) for k in "yn" for s in (0, 1) for c in range(4)]
 SEMAPHORES = ["cv", "cs", "ct", "cg", "sent"] + ["d_" + n for n in DMAS] + ["a_" + n for n in ARRS]
 
-NORM = {"s": "gx0 gx1 gx23 sg0 sg1 cpN0 sg2 cpN1 sa0 cpN2 sg3 sa1 cpN3 cpA3 sa23",
-        "v": "gy0 w0 gy1 wv0 w1 gy2 w2 wv1 gy3 wv2 w3 wv3 vpA0 sb0 vpA1 sb1 vpA2 sb2 sb3",
-        "t": "Xa0 Xa1 Xa2 Xa3 Dw0 Dv0 Dw1 Dw2 Dv1 NB0 Dv2 NB1 Dw3 NB2 Dv3 Np3 NA3 NB3 Z0 pV0 pV1 pV2 Z1 pV3"}
-EDGE = {"s": "gx0 gx1 gx23 sg0 sg1 cpN0 cpN1 sg2 sg3 cpN2 cpN3 sa01 sa23",
-        "v": "gy0 gy1 w0 w1 wv0 wv1 gy2 gy3 w2 w3 wv2 nb0 wv3 nb1 omA vpA0 omB nb2 vpA1 nb3 vpA2 vpA3 rs0 rs1 rs2 rs3",
-        "t": "Xa0 Xa1 Dw0 Dw1 Dv0 Xa2 Xa3 Dv1 NB0 Dw2 NB1 Dw3 Dv2 Dv3 NB2 NB3 pV0 Z0 Z1 pV1 pV2 pV3",
-        "g": "sd0 sd1 sd2 sd3"}
+KIND = ["first", "edge", "norm", "edge", "norm", "last"]
+ONLY = {"id1": 1, "iw1": 1, "off1": 1, "blk2": 2}
 PLAN = {
-    "npre": 4, "ch": [0, 256, 512, 768, 1024], "nd": 3,
+    "up": 0.0, "npre": 4, "nl": 128, "ch": [0, 256, 512, 768, 1024],
     "start": {
-        "y": "Lzo Lnd Lnw Lwl1 Ldl1 Ldr1 Lzr",
-        "s": "Ldl0 Ldr0 Lwl0 Lwt",
-        "g": "pi sel j1 jm eye tri up",
-        "v": "ones pj zw0 icol icb e15 ne zc j9 t2 lx t2b om0 id0 iw0 t1 om1 triw0 onew0 t3 zw1 sm om2 om3 triw1 onew1 triw2 onew2",
-        "t": "zb0 zb1 V0 V1 XO0 XO1 V2 V3 zb2 XO2 XO3 zb3",
+        "y": "Lzo Ldr Lnd Lnw Lwl1 Ldl1 Lzr",
+        "s": "Ldl0 Lwl0 Lwt",
+        "g": "pi sel j1 jm eye pw up off0",
+        "v": "ones vp1 pj zw0 pw0 vp0 padv pads icol e15 icb om0 id0 iw0 j9 lx om1 hp hn r0 r1 zw1 om2 vT vf0 om3 rw0 rw1 rw2",
+        "t": "zb0 zb1 zb2 vT0 vT1 vT2 XO0 zb3 XO1 XO2 XO3",
     },
-    0: {"s": "gx01 gx23 conv sg0 cpN0 sg1 sa0 cpN1 sg2 sg3 cpN2 sa1 cpN3 cpA3 sa23",
-        "v": "gy0 w0 gy1 wv0 w1 gy2 wv1 gy3 w2 w3 iw1 vpA0 wv2 wv3 sb0 vpA1 sb1 vpA2 sb2 id1 sb3",
-        "t": "Xa0 Xa1 Xa2 Xa3 Dw0 Dv0 Dw1 NB0 Dv1 Dw2 Dw3 NB1 Dv2 Dv3 NB2 Np3 NA3 NB3 pV0 Z0 pV1 pV2 Z1 pV3",
-        "g": "off blk"},
-    1: EDGE,
-    2: dict(NORM, g="blk"),
-    3: EDGE,
-    4: NORM,
-    5: {"s": "gx0 gx1 gx23 sg0 cpN0 sg1 sg2 cpN1 cpN2 sg3 sa0 cpN3 zcp Syz cpA3 sa1 sa23",
-        "v": "gy0 gy1 w0 wv0 w1 gy2 wv1 gy3 w2 w3 wv2 wv3 vpA0 sb0 sb1 vpA1 sb2 sb3 vpA2 fin0 fin1",
-        "t": "Xa0 Xa1 Dw0 Dv0 Xa2 Xa3 Dw1 NB0 Dw2 Dv1 Dv2 NB1 Dw3 NB2 Dv3 Np3 Z0 NA3 NB3 Z1",
-        "y": "Syw Syd0 Syd1"},
+    "first": {
+        "g": "blk1",
+        "s": "gx012 gx3 vf conv cm0 cm1 cN0 cN1 sa0 sa1 cN2 cN3 cA2 sa23",
+        "t": "Xa0 Xa1 Xa2 Xa3 Dt0 Dt1 Dt2 bk0 bk1 Dt3 Np2 bk2 bk3 NA2 Z0 XO0 XO1 XO2 Z1 XO3",
+        "v": "gy0 gy1 w0 w1 gy2 w2 sc0 sc1 gy3 w3 sc2 vA0 vA1 vc2 sc3 vc3 sb01 vA3 sb23",
+    },
+    "edge": {
+        "g": "sy0123 sn0 sn1 sn23 off1",
+        "s": "gx0 vf gx1 gx2 gx3 cN0 cm1 cm2 cN1 cN2 cN3 sa0 sa123",
+        "t": "Xa0 Xa1 Dt0 Xa2 Xa3 Dt1 bk0 Dt2 Dt3 bk1 bk2 bk3 Z0 Z1 XO0 XO1 XO2 XO3",
+        "v": "gy01 gy2 w0 gy3 w1 sc0 vc0 w2 w3 sc1 omA sc2 vA0 sc3 vc3 omB iw1 vA1 vA2 id1 vA3 rs0 rs1 rs23",
+    },
+    "norm": {
+        "g": "blk2",
+        "s": "gx0 gx12 gx3 vf cm0 cm1 cN0 cN1 cm2 sa0 cN2 sa1 cN3 cA2 cA3 sa23",
+        "t": "Xa0 Xa1 Xa2 Xa3 Dt0 Dt1 Dt2 bk0 bk1 Dt3 bk2 Np3 bk3 Np2 NA2 XO0 NA3 Z0 XO1 XO2 XO3 Z1",
+        "v": "gy0 gy1 w0 w1 gy2 w2 sc0 sc1 gy3 w3 sc2 vA0 vA1 sc3 vc3 sb01 sb2 sb3",
+    },
+    "last": {
+        "s": "gx0 gx1 gx2 gx3 cN0 cm1 sa0 cN1 cN2 cm3 sa1 cN3 cA3 sa3 sa2 zcp",
+        "t": "Xa0 Xa1 Dt0 Xa2 Dt1 Xa3 bk0 Dt2 Dt3 bk1 bk2 Z0 Np3 bk3 NA3 Z1",
+        "v": "gy01 gy2 w0 w1 gy3 sc0 vc0 w2 sc1 w3 vA0 sc2 vc2 sb0 sc3 vA1 sb12 sb3 vA2 fin0 fin1",
+        "y": "Syw Syz Syd0 Syd1",
+    },
 }
 
 
@@ -63,24 +72,27 @@ def build(T, topo, core, g, plan):
     neng = len(topo.engines(core, dst))
     nin = len(topo.engines(T.cores[(r + 1) % n], core))
     V, S, P = g.vector, g.scalar, g.tensor
-    queues = {"y": [], "s": [], "g": [], "v": [], "t": [], "x": []}
+    queues = {"y": [], "s": [], "g": [], "v": [], "t": []}
     full = lambda b: (b, 0, 1 << 20)
 
     def add(q, name, fn, R, Wr, needs, gives=None, kind="c"):
         R = [full(x) if isinstance(x, str) else x for x in R]
         Wr = [full(x) if isinstance(x, str) else x for x in Wr]
-        queues[q].append({"q": q, "name": name, "fn": fn, "R": R, "W": Wr, "gives": gives or [name], "needs": needs, "kind": kind})
+        queues.setdefault(q, []).append({"q": q, "name": name, "fn": fn, "R": R, "W": Wr, "gives": gives or [name], "needs": needs, "kind": kind})
 
     def dma(q, name, pairs, R, Wr, needs=()):
         eng = g.sync if q == "y" else g.scalar
         add(q, name, lambda: [eng.dma_start(o, i) for o, i in pairs], R, Wr, list(needs), kind="d")
 
-    def remote(name, out, in_, R, Wr, needs):
+    def remote(name, out, in_, R, Wr, needs, gives):
         add("g", name, lambda: g.remote_dma(out, in_, T.sem["a_" + name], T.sem.sent, pid, rid, mask), R, [], needs, ["s_" + name], "r")
-        add("x", name, None, [], Wr, [], ["a_" + name], "a")
+        add("x" + name, name, None, [], Wr, ["s_" + name], gives, "a")
 
-    def asel(name, rows, pat, op, base, cm, src):
-        add("g", name, lambda: g.affine_select(T[name][0:rows, :], T[src][0:rows, :], pat, op, 0.0, base, cm), [src], [name], [src])
+    def asel(name, out, src, pat, op, base, cm, R, Wr):
+        add("g", name, lambda: g.affine_select(out, src, pat, op, 0.0, base, cm), R, Wr, R)
+
+    def fill(name, out, x, Wr, needs=()):
+        add("v", name, lambda: V.memset(out, x), [], Wr, list(needs))
 
     def ts(name, out, in0, s1, s2, ops, R, Wr, needs, gives=None):
         add("v", name, lambda: V.tensor_scalar(out, in0, s1, s2, *ops), R, Wr, needs, gives)
@@ -91,177 +103,184 @@ def build(T, topo, core, g, plan):
     def cp(name, out, in_, R, Wr, needs, gives=None):
         add("v", name, lambda: V.tensor_copy(out, in_), R, Wr, needs, gives)
 
-    def mm(name, out, lhsT, rhs, start, stop, R, Wr, needs, gives=None):
-        add("t", name, lambda: P.matmul(out, lhsT, rhs, start, stop), R, Wr, needs, gives)
+    def mm(name, calls, R, Wr, needs, gives=None):
+        add("t", name, lambda: [P.matmul(*c) for c in calls][-1], R, Wr, needs, gives)
 
     def act(name, out, in_, f, bias, R, Wr, needs, gives=None):
-        if bias: add("s", name, lambda: S.activation(out, in_, f, bias=bias), R, Wr, needs, gives)
-        else: add("s", name, lambda: S.activation(out, in_, f), R, Wr, needs, gives)
+        if bias is None: add("s", name, lambda: S.activation(out, in_, f), R, Wr, needs, gives)
+        else: add("s", name, lambda: S.activation(out, in_, f, bias=bias), R, Wr, needs, gives)
+
+    def plus(q, name, out, in_, bias, R, Wr, needs, gives=None):
+        if q == "s": act(name, out, in_, AF.Identity, bias, R, Wr, needs, gives)
+        elif bias is None: cp(name, out, in_, R, Wr, needs, gives)
+        else: ts(name, out, in_, bias, None, [ALU.add], R, Wr, needs, gives)
 
     col = lambda k: T.cols[:, 4 * k:4 * k + 1]
     cr = lambda k: ("cols", k, k + 1)
-    npre, CH, ND = plan["npre"], plan["ch"], plan["nd"]
+    npre, NL, CH, UP = plan["npre"], plan["nl"], plan["ch"], plan["up"]
     NC = len(CH) - 1
-    ab = lambda m, c: "A%d" % ((m * NC + c) % 4)
-    db = lambda m, c: ("D0", "D1", "ZB")[(m * NC + c) % ND]
-    back = lambda m, c, k: divmod(m * NC + c - k, NC)
-    zb_bank = lambda k: ("D0", "D1", "ZB")[k % 3]
+    db = lambda m, c: "D%d" % ((m * NC + c) % 3)
+    zb_bank = lambda k: "D%d" % (k % 3)
     last = lambda kk, m=M - 1: ["%s%d_%d" % (kk, m, c) for c in range(NC)]
-    oms = lambda a, b: ["om%d" % (a // 512), "om%d" % ((b - 1) // 512)]
-
-    def pre(m, c, which):
-        A = ab(m, c); k = CH[c + 1] - CH[c]; t0 = m * TK + CH[c]
-        prev = ["cpA%d_%d" % back(m, c, 4), "cpN%d_%d" % back(m, c, 4)] if m * NC + c >= 4 else []
-        if prev and back(m, c, 4)[0] in (1, 3): prev.append("nb%d_%d" % back(m, c, 4))
-        if "V" in which:
-            mm("V%d_%d" % (m, c), T[A][:, C:C + k], T.sel[0:8, :], T.vt[0:8, t0:t0 + k], True, True,
-               ["sel", ("vt", t0, t0 + k)], [A], ["sel", "dr0" if m == 0 else "dr1"] + prev)
-        if "X" in which:
-            mm("XO%d_%d" % (m, c), T[A][:, 0:k], T.lx[:, :], T.om[:, t0:t0 + k], True, False,
-               ["lx", ("om", t0, t0 + k)], [A], ["V%d_%d" % (m, c), "lx"] + oms(t0, t0 + k))
+    oms = lambda a, b: ["om%d" % k for k in range(a // 512, (b - 1) // 512 + 1)]
+    lists = lambda m, k: [k + ("0" if m * 64 < NL else "1")]
 
     def fixed(q, w, m):
         if w == "Lzo": dma(q, "zo", [(T.zt[0:8, 0:npre * 512], T.zo[:, 0:npre * 512])], [], ["zt"])
         elif w == "Lzr": dma(q, "zr", [(T.zr[i:128:16, npre * 512:], T.zo[:, npre * 512:]) for i in range(16)], [], ["zr"])
-        elif w == "Ldr0": dma(q, "dr0", [(T.vt[0:8, 0:TK], T.dr[:, 0:TK])], [], [("vt", 0, TK)])
-        elif w == "Ldr1": dma(q, "dr1", [(T.vt[0:8, TK:], T.dr[:, TK:])], [], [("vt", TK, M * TK)])
+        elif w == "Ldr": dma(q, "dr", [(T.vt[:, :], T.dr[:, :])], [], ["vt"])
         elif w[:3] in ("Ldl", "Lwl"):
-            a, b = ((0, 64), (64, 384))[int(w[3])]
+            a, b = ((0, NL), (NL, 384))[int(w[3])]
             dma(q, w[1:], [(T[w[1:3] + "i"][:, a:b], T[w[1:3]][:, a:b])], [], [(w[1:3] + "i", a, b)])
         elif w[:2] in ("id", "iw"):
-            a, b = ((0, 64), (64, 384))[int(w[2])]
+            a, b = ((0, NL), (NL, 384))[int(w[2])]
             k = w[1] + "l"
             cp(w, T[k + "u"][:, a:b], T[k + "i"][:, a:b], [(k + "i", a, b)], [(k + "u", a, b)], [k + w[2]])
         elif w == "Lwt": dma(q, "wt", [(T.wts[:, 0:3], T.wt[:, :])], [], ["wts"])
         elif w == "Lnd": dma(q, "nd", [(T.ndb[:, :], T.nd[:, :])], [], ["ndb"])
         elif w == "Lnw": dma(q, "nw", [(T.W0[:, :], T.nw[:, :])], [], ["W0"])
         elif w == "pi": add(q, w, lambda: g.iota(T.pi[:, 0:1], [[0, 1]], 0, 1), [], [w], [])
-        elif w == "sel": asel(w, 8, [[1, 8], [0, 16]], ALU.is_equal, 0, -1, "ones")
-        elif w == "j1": asel(w, 128, [[-16, 8], [0, 16]], ALU.is_ge, 0, 1, "ones")
-        elif w == "jm": asel(w, 128, [[16, 8], [0, 16]], ALU.is_ge, 15, -1, "j1")
-        elif w == "tri": asel(w, 128, [[1, 128]], ALU.is_ge, 0, -1, "j1")
-        elif w == "eye": asel(w, 128, [[1, 128]], ALU.is_equal, 0, -1, "ones")
-        elif w == "up": asel(w, 128, [[1, 128]], ALU.is_equal, -1, -1, "j1")
-        elif w == "ones": add(q, w, lambda: V.memset(T.ones[:, :], 1.0), [], [w], [])
-        elif w == "zw0": add(q, w, lambda: V.memset(T.zw[:, :], 0.0), [], ["zw"], [])
+        elif w == "sel": asel(w, T.sel[0:8, :], T.ones[0:8, 0:B], [[1, 8], [0, 16]], ALU.is_equal, 0, -1, ["ones"], [w])
+        elif w == "j1": asel(w, T.j1[:, :], T.ones[:, 0:B], [[-16, 8], [0, 16]], ALU.is_ge, 0, 1, ["ones"], [w])
+        elif w == "jm": asel(w, T.jm[:, :], T.j1[:, :], [[16, 8], [0, 16]], ALU.is_ge, 15, -1, ["j1"], [w])
+        elif w == "eye": asel(w, T.eye[:, :], T.ones[:, 0:B], [[1, B]], ALU.is_equal, 0, -1, ["ones"], [w])
+        elif w == "up": asel(w, T.up[:, :], T.j1[:, :], [[1, B]], ALU.is_equal, -1, -1, ["j1"], [w])
+        elif w == "pw": asel(w, T.pw[:, 16:400], T.ones[:, :], [[1, 16], [1000, 3], [16, 8]], ALU.is_equal, 0, -1, ["ones"], [("pw", 16, 400)])
+        elif w == "ones": fill(w, T.ones[:, :], 1.0, [w])
+        elif w == "zw0": fill(w, T.zw[:, :], 0.0, ["zw"])
+        elif w == "pw0": fill(w, T.pw[:, 0:16], 0.0, [("pw", 0, 16)])
+        elif w == "vp1": fill(w, T.vp[:, :], 1.0, ["vp"])
+        elif w == "vp0": fill(w, T.vp[:, 0:2 * TK:16], 0.0, ["vp"], ["vp1"])
+        elif w == "padv": fill(w, T.cv[:, :], 2.0, ["cv"])
+        elif w == "pads": fill(w, T.cs[:, :], 1.0, ["cs"])
         elif w == "pj": ts(w, T.pj[:, 0:1], T.pi[:, 0:1], 15, None, [ALU.bitwise_and], ["pi"], [w], ["pi"])
         elif w == "icol": cp(w, col(0), T.pj[:, 0:1], ["pj"], [cr(0)], ["pj"])
         elif w == "icb": cp(w, T.icb[:, 0:1], col(0), [cr(0)], [w], ["icol"])
-        elif w == "e15": ts(w, col(1), col(0), 15.0, None, [ALU.is_equal], [cr(0)], [cr(1)], ["icol"])
-        elif w == "ne": ts(w, col(2), col(1), -1.0, None, [ALU.mult], [cr(1)], [cr(2)], ["e15"])
-        elif w == "zc": ts(w, col(3), col(1), 8.0, -0.5, [ALU.mult, ALU.add], [cr(1)], [cr(3)], ["e15"])
+        elif w == "e15": ts(w, col(1), col(0), 15.0, -1.0, [ALU.is_equal, ALU.add], [cr(0)], [cr(1)], ["icol"])
         elif w == "j9": ts(w, T.t3[:, :], T.jm[:, :], -9.0, None, [ALU.mult], ["jm"], ["t3"], ["jm"])
         elif w == "lx": tt(w, T.lx[:, :], T.t3[:, :], T.eye[:, :], ALU.add, ["t3", "eye"], [w], ["j9", "eye"])
-        elif w == "t1": tt(w, T.t1[:, :], T.eye[:, :], T.up[:, :], ALU.subtract, ["up", "eye"], [w], ["up", "eye"])
-        elif w == "t2": ts(w, T.t2[:, :], T.jm[:, :], col(2), None, [ALU.mult], ["jm", cr(2)], [w], ["jm", "ne"])
-        elif w == "t2b": ts(w, T.t2[:, 0:128:16], T.t2[:, 0:128:16], 0.5, None, [ALU.mult], ["t2"], ["t2"], ["t2"])
-        elif w == "t3": ts(w, T.t1[:, :], T.t1[:, :], 0.5, None, [ALU.mult], ["t1"], ["t1"], ["t1"])
-        elif w == "sm": tt(w, T.sm[:, :], T.t1[:, :], T.t2[:, :], ALU.add, ["t1", "t2"], [w], ["t3", "t2b"])
-        elif w == "zw1": ts(w, T.zw[:, 11:96:12], T.jm[:, 0:128:16], col(3), None, [ALU.mult], ["jm", "zw", cr(3)], ["zw"], ["jm", "zc", "zw0"])
-        elif w[:4] in ("triw", "onew"):
-            h = int(w[4]); src, k = ("tri", 32.0) if w[0] == "t" else ("jm", -1.0)
-            ts(w, T[w[:4]][:, h * 128:(h + 1) * 128], T[src][:, :], T.wts[:, h:h + 1], k, [ALU.mult, ALU.mult], [src, "wts"], [(w[:4], h, h + 1)], [src, "wt"])
+        elif w == "r0": ts(w, T.r0[:, :], T.up[:, :], -32.0, None, [ALU.mult], ["up"], [w], ["up"])
+        elif w == "r1": cp(w, T.r0[:, 0:B:16], T.jm[:, 0:B:16], ["jm"], ["r0"], ["jm", "r0"])
+        elif w in ("hp", "hn"): ts(w, T[w][:, :], T.eye[:, :], 0.5 if w == "hp" else -0.5, None, [ALU.mult], ["eye"], [w], ["eye"])
+        elif w == "zw1": ts(w, T.zw[:, 11:96:12], T.jm[:, 0:B:16], col(0), None, [ALU.mult], ["jm", "zw", cr(0)], ["zw"], ["jm", "icol", "zw0"])
+        elif w[:2] == "rw":
+            h = int(w[2])
+            ts(w, T.rw[:, h * B:(h + 1) * B], T.r0[:, :], T.wts[:, h:h + 1], None, [ALU.mult], ["r0", "wts"], [("rw", h, h + 1)], ["r1", "wt"])
         elif w[:2] == "zb":
             k = int(w[2:]); b = zb_bank(k)
-            mm(w, T[b][:, 0:512], T.sel[0:8, :], T.zt[0:8, k * 512:(k + 1) * 512], True, True, ["sel", "zt"], [b], ["sel", "zo"] + (["om%d" % (k - 3)] if k >= 3 else []))
+            mm(w, [(T[b][:, 0:512], T.sel[0:8, :], T.zt[0:8, k * 512:(k + 1) * 512], True, True)], ["sel", "zt"], [b], ["sel", "zo"] + (["om%d" % (k - 3)] if k >= 3 else []))
+        elif w in ("vT0", "vT1", "vT2"):
+            c = int(w[2])
+            mm(w, [(T.ZZ[:, 0:384], T.vt[:, c * B:(c + 1) * B], T.pw[:, 16 - 8 * c:400 - 8 * c], c == 0, c == 2)], ["vt", "pw"], ["ZZ"], ["dr", "pw", "pw0"] + (["vT%d" % (c - 1)] if c else []))
+        elif w == "vT": plus(q, w, T.vT[:, :], T.ZZ[:, 0:384], None, ["ZZ"], [w], ["vT2"])
+        elif w[:2] == "vf":
+            k = int(w[2:]) if w[2:] else m + 1
+            a = (k % 2) * TK
+            plus(q, "vf%d" % k, T.vp[:, a + 1:a + TK:16], T.vT[:, k * 64:(k + 1) * 64], None, ["vT"], [("vp", a, a + TK)], ["vT", "vp0"] + (last("sc", k - 2) if k >= 2 else []))
         elif w in ("omA", "omB"):
             k = 2 * (m + 1 + "AB".index(w[2])); a = k * 512
             ts(w, T.om[:, a:a + TK], T.zr[:, a:a + TK], T.icb[:, 0:1], None, [ALU.not_equal], ["zr", "icb"], [("om", a, a + TK)], ["zr", "icb"], oms(a, a + TK))
         elif w[:2] == "om":
             k = int(w[2:]); b = zb_bank(k)
             ts(w, T.om[:, k * 512:(k + 1) * 512], T[b][:, 0:512], col(0), None, [ALU.not_equal], [b, cr(0)], [("om", k * 512, (k + 1) * 512)], ["zb%d" % k, "icol"])
-        elif w[:2] == "XO": pre(0, int(w[2]), "X")
-        elif w[0] == "V": pre(0, int(w[1]), "V")
-        elif w == "conv": act(w, T.doc[:, :], T.ndb[:, :], AF.Silu, 0, ["ndb"], ["doc"], ["nd"])
-        elif w == "off": remote(w, T.nbo[:, :], T.wlu[:, 64:256], [("wlu", 64, 256)], ["nbo"], ["iw1"])
-        elif w == "blk":
+        elif w == "conv": act(w, T.doc[:, :], T.ndb[:, :], AF.Silu, UP, ["ndb"], ["doc"], ["nd"])
+        elif w[:3] == "off":
+            h = int(w[3]); a = (2 * h + 1) * 64
+            remote(w, T.nbo[:, h * 64:h * 64 + 64], T.wlu[:, a:a + 64], [("wlu", a, a + 64)], [("nbo", h, h + 1)], lists(2 * h + 1, "iw"), ["a_" + w])
+        elif w[:3] == "blk":
             a, b = "W%d" % (m // 2), "W%d" % (m // 2 + 1)
-            remote("blk" + b[1], T[b][:, :], T[a][:, :], [a], [b], last("sb", m))
+            remote("blk" + b[1], T[b][:, :], T[a][:, :], [a], [b], last("sb", m), ["a_blk" + b[1]])
         elif w == "Syw": dma(q, "yw", [(T.yw[:, :], T.W2[:, :])], ["W2"], [], last("sb"))
         elif w[:3] == "fin":
             a = int(w[3]) * TK
-            ts(w, T.ydb[:, a:a + TK], T.doc[:, a:a + TK], MAGIC, MAGIC, [ALU.add, ALU.subtract], ["doc"], [("ydb", a, a + TK)], last("sa"))
+            if q == "v": ts(w, T.ydb[:, a:a + TK], T.doc[:, a:a + TK], MAGIC - UP, MAGIC, [ALU.add, ALU.subtract], ["doc"], [("ydb", a, a + TK)], last("sa"))
+            else: act(w, T.ydb[:, a:a + TK], T.doc[:, a:a + TK], AF.Relu, -UP - 2.0 ** -10, ["doc"], [("ydb", a, a + TK)], last("sa"))
         elif w[:3] == "Syd":
             a = int(w[3]) * TK
             dma(q, w[1:], [(T.yd[:, a:a + TK], T.ydb[:, a:a + TK])], [("ydb", a, a + TK)], [], ["fin" + w[3]])
-        elif w == "zcp": act(w, T.zs[0:96, :], T.ZZ[0:96, 0:512], AF.Identity, 0, ["ZZ"], ["zs"], ["Z5_1"])
+        elif w == "zcp": plus(q, w, T.zs[0:96, :], T.ZZ[0:96, 0:512], 120.0, ["ZZ"], ["zs"], ["Z5_1"])
         elif w == "Syz": dma(q, "yz", [(T.yz[:, :], T.zs[0:96, :])], ["zs"], [], ["zcp"])
         else: return False
         return True
 
-    def chunk(m, w):
-        h = m // 2
+    def chunk(q, m, w):
         k = w.rstrip("0123456789")
         cs = [int(x) for x in w[len(k):]]
+        if k == "XO": m = 0 if m == "start" else m + 1
+        h = m // 2
         tag = lambda kk, cc=None, mb=m: ["%s%d_%d" % (kk, mb, c) for c in (cs if cc is None else cc)]
-        c0 = cs[0]; a, b = CH[c0], CH[cs[-1] + 1]; u = min(b - a, C)
+        c0 = cs[0]; a, b = CH[c0], CH[cs[-1] + 1]; u = b - a
         t0, t1 = m * TK + a, m * TK + b
         o0, o1 = t0 // 16, t1 // 16
         e0, e1 = h * TK + a, h * TK + b
         s0, s1 = (m % 2) * TK + a, (m % 2) * TK + b
-        A = ab(m, c0); Dk = db(m, c0); Wk = "W%d" % h
-        lo, hi, dd = T[A][:, 0:u], T[A][:, C:C + u], T[Dk][:, 0:u]
+        p0 = a + c0 * PAD
+        X = "X%d" % c0; Dk = db(m, c0); Wk = "W%d" % h
         name = "%s_%d" % (w, m)
         me = tag(k)
-        byact = ("cpA%d" % c0) in plan[m]["s"].split()
+        blocks = range(0, u, B)
         wordw = lambda: T[Wk][:, 0:W].indirect(T.wlu[:, o0:o1])
         if k == "gx":
-            src, prev = ("ndb", ["nd", "id0"]) if m == 0 else ("doc", last("sa", m - 1) + ["id1"])
-            act(name, T.ag[:, a:b], T[src][:, 0:D].indirect(T.dlu[:, o0:o1]), AF.Identity, OFF, [src, ("dlu", o0, o1)], [("ag", a, b)], prev, me)
+            src, prev, bias = ("ndb", ["nd"], OFF) if m == 0 else ("doc", last("sa", m - 1), OFF - UP)
+            act(name, T.ag[:, a:b], T[src][:, 0:D].indirect(T.dlu[:, o0:o1]), AF.Identity, bias, [src, ("dlu", o0, o1)], [("ag", a, b)], prev + lists(m, "id"), me)
         elif k == "gy":
-            prev = ["nw", "iw0"] if m == 0 else last("sb", m - 1) + ["iw1"]
-            tt(name, T.y1[:, a:b], wordw(), T.om[:, t0:t1], ALU.add, [Wk, ("wlu", o0, o1), ("om", t0, t1)], [("y1", a, b)], prev + oms(t0, t1), me)
-        elif k == "Xa": mm(name, lo, T.eye[:, :], T.ag[:, a:b], False, True, ["eye", ("ag", a, b)], [A], tag("XO") + tag("gx"), me)
-        elif k == "w": tt(name, T.wp[:, a:b], lo, T.y1[:, a:b], ALU.mult, [A, ("y1", a, b)], [("wp", a, b)], tag("Xa") + tag("gy"), me)
-        elif k == "wv": tt(name, T.wv[:, a:b], hi, T.wp[:, a:b], ALU.mult, [A, ("wp", a, b)], [("wv", a, b)], tag("w"), me)
-        elif k == "Dw":
-            if m * NC + c0 >= ND: prev = ["sg%d_%d" % back(m, c0, ND)]
-            else: prev = ["om%d" % j for j in range(npre) if zb_bank(j) == Dk]
-            mm(name, dd, T.triw[:, h * 128:(h + 1) * 128], T.wp[:, a:b], True, False,
-               [("triw", h, h + 1), ("wp", a, b)], [Dk], tag("w") + prev + ["triw%d" % h], me)
-        elif k == "Dv":
-            mm(name, dd, T.onew[:, h * 128:(h + 1) * 128], T.wv[:, a:b], False, True,
-               [("onew", h, h + 1), ("wv", a, b)], [Dk], tag("Dw") + tag("wv") + ["onew%d" % h], me)
-        elif k == "sg": act(name, T.sg[:, s0:s1], dd, AF.Sign, -0.5, [Dk], [("sg", s0, s1)], tag("Dv") + (["Z%d_1" % (m - 2)] if m >= 2 else []), me)
+            prev = ["nw"] if m == 0 else last("sb", m - 1)
+            tt(name, T.y1[:, t0:t1], wordw(), T.om[:, t0:t1], ALU.add, [Wk, ("wlu", o0, o1), ("om", t0, t1)], [("y1", t0, t1)], prev + oms(t0, t1) + lists(m, "iw"), me)
+        elif k == "XO":
+            mm(name, [(T[X][:, 0:u], T.lx[:, :], T.om[:, t0:t1], True, False)], ["lx", ("om", t0, t1)], [X], ["lx"] + oms(t0, t1) + (tag("cA", None, m - 1) if m else []), me)
+        elif k == "Xa": mm(name, [(T[X][:, 0:u], T.eye[:, :], T.ag[:, a:b], False, True)], ["eye", ("ag", a, b)], [X], tag("XO") + tag("gx"), me)
+        elif k == "w": tt(name, T.wp[:, a:b], T[X][:, 0:u], T.y1[:, t0:t1], ALU.mult, [X, ("y1", t0, t1)], [("wp", a, b)], tag("Xa") + tag("gy"), me)
+        elif k == "Dt":
+            j = m * NC + c0
+            prev = ["cN%d_%d" % divmod(j - 3, NC)] if j >= 3 else ["om%d" % i for i in range(npre) if zb_bank(i) == Dk]
+            mm(name, [(T[Dk][:, j:j + B], T.wp[:, a + j:a + j + B], T.rw[:, h * B:(h + 1) * B], True, True) for j in blocks],
+               [("rw", h, h + 1), ("wp", a, b)], [Dk], tag("w") + prev + ["rw%d" % h], me)
+        elif k == "sc":
+            add(q, name, lambda: V.tensor_tensor_scan(T.ee[:, a:b], T.vp[:, s0:s1], T[Dk][:, 0:u], 0.0, ALU.mult, ALU.add),
+                [Dk, ("vp", s0, s1)], [("ee", a, b)], tag("Dt") + ["vf%d" % m], me)
+        elif k == "vc": ts(name, T.cv[:, p0:p0 + u], T.ee[:, a:b], 0.0, 2.0, [ALU.is_ge, ALU.mult], [("ee", a, b)], [("cv", p0, p0 + u)], tag("sc") + ["padv"], tag("cm"))
+        elif k == "cm": act(name, T.cs[:, p0:p0 + u], T.ee[:, a:b], AF.Sign, 0.5, [("ee", a, b)], [("cs", p0, p0 + u)], tag("sc") + ["pads"], me)
+        elif k == "bk":
+            c = "cv" if ("vc%d" % c0) in plan[KIND[m]]["v"].split() else "cs"
+            mm(name, [(T[Dk][:, j:j + B], T[c][:, p0 + j + i:p0 + j + i + B], T[("hp", "hn")[i]][:, :], i == 0, i == 1) for j in blocks for i in (0, 1)],
+               ["hp", "hn", (c, p0, p0 + u + PAD)], [Dk], tag("cm") + ["hp", "hn"], me)
+        elif k == "cN": plus(q, name, T.nm[:, t0:t1], T[Dk][:, 0:u], col(1), [Dk, cr(1)], [("nm", t0, t1)], tag("bk") + ["e15"], me)
         elif k == "Np":
-            mm(name, lo, T.eye[:, :], T.om[:, t0:t1], True, False, ["eye", ("om", t0, t1)], [A], tag("wv"))
-            mm(name + "a", lo, T.eye[:, :], T.ag[:, a:b], False, False, ["eye", ("ag", a, b)], [A], [], me)
-        elif k == "NA": mm(name, lo, T.sm[:, :], T.sg[:, s0:s1], False, True, ["sm", ("sg", s0, s1)], [A], tag("sg") + tag("Np") + ["sm"], me)
-        elif k == "NB": mm(name, hi, T.sm[:, :], T.sg[:, s0:s1], True, True, ["sm", ("sg", s0, s1)], [A], tag("NA" if byact else "sg") + ["sm"], me)
-        elif k == "cpA": act(name, T.na[:, a:b], lo, AF.Identity, -OFF, [A], [("na", a, b)], tag("NB"), me)
-        elif k == "cpN": act(name, T.nm[:, a:b], hi, AF.Identity, 0, [A], [("nm", a, b)], tag("NB"), me)
-        elif k == "vpA": tt(name, T.na[:, a:b], lo, T.nm[:, a:b], ALU.add, [A, ("nm", a, b)], [("na", a, b)], tag("cpN"), tag("cpA"))
-        elif k == "nb":
-            tt(name, T.nsend[:, e0:e1], hi, T.y1[:, a:b], ALU.add, [A, ("y1", a, b)], [("nsend", e0, e1)], tag("NB"),
-               me + ([] if ("cpN%d" % c0) in plan[m]["s"].split() else tag("cpN")))
+            mm(name, [(T[X][:, 0:u], T.lx[:, :], T.om[:, t0:t1], True, False), (T[X][:, 0:u], T.eye[:, :], T.ag[:, a:b], False, False)],
+               ["lx", "eye", ("om", t0, t1), ("ag", a, b)], [X], tag("w"), me)
+        elif k == "NA": mm(name, [(T[X][:, 0:u], T.eye[:, :], T.nm[:, t0:t1], False, True)], ["eye", ("nm", t0, t1)], [X], tag("cN") + tag("Np"), me)
+        elif k == "cA": plus(q, name, T.na[:, a:b], T[X][:, 0:u], UP, [X], [("na", a, b)], tag("NA"), me)
+        elif k == "vA": tt(name, T.na[:, a:b], T[X][:, 0:u], T.nm[:, t0:t1], ALU.add, [X, ("nm", t0, t1)], [("na", a, b)], tag("cN"), tag("cA"))
         elif k == "sa":
-            act(name, T.doc[:, 0:D].indirect(T.dlu[:, o0:o1]), T.na[:, a:b], AF.Silu, 0, [("na", a, b), ("dlu", o0, o1)], ["doc"],
-                tag("cpA") + last("gx", m) + ["conv"], me)
+            act(name, T.doc[:, 0:D].indirect(T.dlu[:, o0:o1]), T.na[:, a:b], AF.Silu, None, [("na", a, b), ("dlu", o0, o1)], ["doc"],
+                tag("cA") + ["conv"], me)
         elif k == "sb":
-            tt(name, wordw(), T.y1[:, a:b], T.nm[:, a:b], ALU.add, [("y1", a, b), ("nm", a, b), ("wlu", o0, o1)], [Wk], tag("cpN") + last("gy", m), me)
-        elif k == "sd": remote("val%d_%d" % (h, c0), T.nrecv[:, e0:e1], T.nsend[:, e0:e1], [("nsend", e0, e1)], [("nrecv", e0, e1)], tag("nb"))
+            tt(name, wordw(), T.y1[:, t0:t1], T.nm[:, t0:t1], ALU.add, [("y1", t0, t1), ("nm", t0, t1), ("wlu", o0, o1)], [Wk], tag("cN"), me)
+        elif k in ("sy", "sn"):
+            src, land = (("y1", "yrecv"), ("nm", "nrecv"))[k == "sn"]
+            remote("%s%d_%d" % (k[1], h, c0), T[land][:, e0:e1], T[src][:, t0:t1], [(src, t0, t1)], [(land, e0, e1)], tag("gy" if k == "sy" else "cN"), tag("a" + k))
         elif k == "rs":
             Wn = "W%d" % (h + 1)
-            cp(name, T[Wn][:, 0:W].indirect(T.nbo[:, o0 - 64:o1 - 64]), T.nrecv[:, e0:e1], [("nrecv", e0, e1), "nbo"], [Wn], [], tag("sb"))
+            tt(name, T[Wn][:, 0:W].indirect(T.nbo[:, h * 64 + a // 16:h * 64 + b // 16]), T.yrecv[:, e0:e1], T.nrecv[:, e0:e1], ALU.add,
+               [("yrecv", e0, e1), ("nrecv", e0, e1), ("nbo", h, h + 1)], [Wn],
+               tag("asy") + tag("asn") + ["a_off%d" % h, "a_blk%d" % (h + 1)], tag("sb"))
         elif k == "Z":
             j = 2 * m + c0
-            z0 = (m % 2) * TK + c0 * 512
-            mm(name, T.ZZ[0:96, 0:512], T.zw[:, 11 - j:107 - j], T.sg[:, z0:z0 + 512], j == 0, j == 11, ["zw", ("sg", z0, z0 + 512)], ["ZZ"],
-               tag("sg", [c for c in range(NC) if CH[c] < c0 * 512 + 512 and CH[c + 1] > c0 * 512]) + ["zw1"] + (["Z%d_%d" % divmod(j - 1, 2)] if j else []), me)
-        elif k == "pV":
-            if m + 1 < M: pre(m + 1, c0, "VX")
+            z0 = m * TK + c0 * 512
+            mm(name, [(T.ZZ[0:96, 0:512], T.zw[:, 11 - j:107 - j], T.nm[:, z0:z0 + 512], j == 0, j == 11)], ["zw", ("nm", z0, z0 + 512)], ["ZZ"],
+               tag("cN", [c for c in range(NC) if CH[c] < c0 * 512 + 512 and CH[c + 1] > c0 * 512]) + ["zw1", "vT"] + (["Z%d_%d" % divmod(j - 1, 2)] if j else []), me)
         else: raise ValueError(w)
 
     for m in ["start"] + list(range(M)):
         for q in "ysvtg":
-            for w in plan[m].get(q, "").split():
-                if not fixed(q, w, m): chunk(m, w)
+            for w in plan[m if m == "start" else KIND[m]].get(q, "").split():
+                if ONLY.get(w, m) == m and not fixed(q, w, m): chunk(q, m, w)
 
     order, have, pos = [], set(), {q: 0 for q in queues}
     moved = True
     while moved:
         moved = False
-        for q in "xysgvt":
+        for q in queues:
             while pos[q] < len(queues[q]) and all(x in have for x in queues[q][pos[q]]["needs"]):
                 o = queues[q][pos[q]]; order.append(o); have.update(o["gives"]); pos[q] += 1; moved = True
     stuck = [(q, queues[q][pos[q]]["name"], [x for x in queues[q][pos[q]]["needs"] if x not in have]) for q in queues if pos[q] < len(queues[q])]

@@ -1,3 +1,4 @@
+from concourse.bass import DstId, RemoteDMATransfer
 from concourse.mybir import AluOpType as ALU, ActivationFunctionType as AF
 
 D, W, H, TK, M = 2048, 4096, 3, 1024, 6
@@ -8,9 +9,10 @@ MAGIC = 12582912.0
 
 SCRATCH = {}
 for _n, _c in (("W0", W), ("W1", W), ("W2", W), ("ndb", D), ("ydb", D), ("zt", M * TK), ("om", M * TK), ("zr", M * TK),
-               ("y1", M * TK), ("nm", M * TK), ("yrecv", 2 * TK), ("nrecv", 2 * TK), ("ag", TK), ("vp", 2 * TK),
+               ("y1", M * TK), ("nm", M * TK), ("yrecv", 2 * TK), ("nrecv", 2 * TK), ("ag", TK), ("vp", 2 * TK), ("nsend", 2 * TK), ("kc", TK),
+               ("zc", 384), ("zc2", 384), ("zq", M * TK), ("m2i", B), ("s2i", B),
                ("ee", TK), ("cv", TK + 8 * PAD), ("cs", TK + 8 * PAD), ("zs", 512), ("zw", 112), ("vt", 384), ("vT", 384), ("pw", 400),
-               ("ones", 384), ("sel", B), ("j1", B), ("jm", B), ("eye", B), ("up", B), ("lx", B), ("hp", B), ("hn", B),
+               ("ones", 384), ("sel", B), ("j1", B), ("jm", B), ("eye", B), ("up", B), ("lx", B), ("hp", B), ("hn", B), ("hq", B), ("hr", B),
                ("r0", B), ("t3", B), ("icb", 8)):
     SCRATCH[_n] = ("sbuf", [128, _c], "bfloat16")
 for _n, _c in (("doc", D), ("wts", 4), ("wp", TK), ("na", TK), ("rw", 384), ("cols", 16)):
@@ -18,17 +20,18 @@ for _n, _c in (("doc", D), ("wts", 4), ("wp", TK), ("na", TK), ("rw", 384), ("co
 for _n, _c, _t in (("dli", 384, "int32"), ("wli", 384, "int32"), ("pi", 4, "int32"), ("pj", 4, "int32"),
                    ("dlu", 384, "uint16"), ("wlu", 384, "uint16"), ("nbo", 128, "uint16")):
     SCRATCH[_n] = ("sbuf", [128, _c], _t)
-BANKS = ("X0", "X1", "X2", "X3", "D0", "D1", "D2", "ZZ")
+BANKS = ("P0", "P1", "P2", "P3", "P4", "P5", "P6", "ZZ")
 for _n in BANKS:
     SCRATCH[_n] = ("psum", [128, 512], "float32")
-DMAS = ["zo", "dl0", "wl0", "dr", "wt", "nd", "nw", "dl1", "wl1", "zr", "yw", "yd0", "yd1", "yz"]
-ARRS = ["off0", "off1", "blk1", "blk2"] + ["%s%d_%d" % (k, s, c) for k in "yn" for s in (0, 1) for c in range(4)]
+DMAS = ["conv", "zc", "zq", "zo", "dl0", "wl0", "dr", "wt", "nd", "nw", "dl1", "wl1", "zr", "yw", "yd0", "yd1", "yz"]
+ARRS = ["off0", "off1", "blk1", "blk2"] + ["%s%d_%d" % (k, s, c) for k in "yn" for s in (0, 1) for c in range(5)]
 SEMAPHORES = ["cv", "cs", "ct", "cg", "sent"] + ["d_" + n for n in DMAS] + ["a_" + n for n in ARRS]
 
 KIND = ["first", "edge", "norm", "edge", "norm", "last"]
 ONLY = {"id1": 1, "iw1": 1, "off1": 1, "blk2": 2}
 PLAN = {
-    "up": 0.0, "npre": 4, "nl": 128, "ch": [0, 256, 512, 768, 1024],
+    "om": {"A1": 2, "B1": 3, "A3": 4, "B3": 5},
+    "gate": 1, "early": 1, "cs": 0, "nz": 4, "nhi": (), "up": 0.0, "npre": 4, "nl": 128, "ch": [0, 256, 512, 768, 1024],
     "start": {
         "y": "Lzo Ldr Lnd Lnw Lwl1 Ldl1 Lzr",
         "s": "Ldl0 Lwl0 Lwt",
@@ -61,6 +64,134 @@ PLAN = {
         "y": "Syw Syz Syd0 Syd1",
     },
 }
+PLAN.update({
+    "start": {
+        "y": "Ldr Lzo Lnd Lnw Lwl1 Ldl1 Lzr",
+        "s": "Lwl0 Lwt Ldl0 r0 r1 j9 rw0 rw2 hn vT zw1 hp rw1 vf0",
+        "g": "pi j1 pw up jm sel eye off0",
+        "v": "ones pads vp1 zw0 iw0 pw0 pj icol padv vp0 icb om0 lx id0 e15 om1 om2 om3",
+        "t": "vT0 vT1 zb0 vT2 zb1 zb2 XO1 zb3 XO0 XO3 XO2",
+    },
+    "first": {
+        "g": "blk1",
+        "s": "gx0123 conv cm1 cN0 cN1 sa0 cN2 sa1 cN3 cA2 sa2 sa3",
+        "t": "Xa2 Xa1 Xa0 Xa3 Dt0 Dt1 Np2 bk0 Dt2 bk1 Dt3 XO0 bk2 Z0 bk3 XO1 NA2 XO3 XO2 Z1",
+        "v": "gy0 gy2 w0 gy1 w1 sc0 w2 vc0 sc1 gy3 vf w3 sc2 vA0 vc2 vA1 sc3 vc3 sb01 vA3 sb23",
+    },
+    "edge": {
+        "g": "sf0 sf1 off1 sf2 sf3",
+        "s": "vf gx0 gx1 gx2 gx3 cm0 cN0 cN1 sa0 cA1 cN3 sa1 cA3 sa2 sa3",
+        "t": "Xa0 Xa1 Dt0 Xa2 Dt1 Xa3 bk0 Dt2 bk1 Dt3 Np1 bk2 Np3 NA1 bk3 XO0 NA3 Z0 XO3 XO2 XO1 Z1",
+        "v": "gy0 gy1 w0 gy2 w1 sc0 w2 gy3 sc1 w3 vc1 omB sc2 vA0 vc2 sc3 iw1 vc3 cN2 id1 omA vA2 rs0 rs1 rs2 rs3",
+    },
+    "norm": {
+        "g": "blk2",
+        "s": "gx0 gx123 cm0 cN0 cN1 sa0 sa1 cA2 cN3 sa2 cA3 sa3",
+        "t": "Xa0 Xa3 Xa2 Xa1 Dt0 Dt1 Dt2 bk0 bk1 Dt3 bk2 Np3 Np2 NA2 bk3 Z0 NA3 XO2 Z1 XO0 XO3 XO1",
+        "v": "vf gy0 gy1 w0 gy2 w1 w2 sc0 gy3 sc1 vc1 w3 sc2 vA0 vc2 vA1 sc3 cN2 vc3 sb01 sb23",
+    },
+    "last": {
+        "s": "gx0 gx1 gx23 cm0 cN0 cm1 sa0 cN2 cA1 cN3 sa1 cA3 cA2 sa23 zcp",
+        "t": "Xa0 Xa1 Dt0 Xa3 Xa2 Dt1 bk0 Dt2 Dt3 bk1 Np1 bk2 Np2 NA1 bk3 Np3 Z0 NA3 Z1 NA2",
+        "v": "gy0 gy1 w0 gy3 w1 sc0 gy2 w2 w3 sc1 vA0 sc2 vc2 sc3 cN1 vc3 sb01 sb23 fin0 fin1",
+        "y": "Syw Syz Syd0 Syd1",
+    },
+})
+PLAN.update({
+    "start": {
+        "y": "Lzo Ldr Lnd Lnw Lwl1 Ldl1 Lzr",
+        "s": "Lwt Lwl0 Ldl0 hp hq hn j9 hr vT r0 vf0 r1 rw0 rw1 rw2 zw1",
+        "g": "pi sel eye j1 pw jm up off0",
+        "v": "ones pads pj vp1 icol padv e15 pw0 vp0 zw0 icb om0 id0 lx om1 iw0 om2 om3",
+        "t": "zb0 zb1 zb2 vT0 vT1 vT2 zb3 XO0 XO1 XO2 XO3",
+    },
+    "first": {
+        "g": "blk1",
+        "s": "gx0 gx12 conv gx3 cA0 cN0 sa0 cm2 sa1 cm3 cA2 cN2 sa2 cA3 sa3",
+        "t": "Xa0 Xa1 Xa2 Dt0 Np0 Dt1 bk0 bA0 Xa3 Dt2 bk1 Dt3 Np2 XO1 Np3 bA2 bk2 bk3 XO2 bA3 Z0 XO3 XO0 Z1",
+        "v": "gy0 w0 gy1 vf w1 sc0 gy3 vc0 gy2 w2 sc1 vc1 w3 sc2 cN1 vA1 sc3 sb01 cN3 sb23",
+    },
+    "edge": {
+        "g": "sy012 sn0 sy3 sn1 sn2 sn3 off1",
+        "s": "gx0 gx1 gx2 gx3 cN0 cm1 cN1 cm2 cm3 sa0 cN3 cA3 sa123",
+        "t": "Xa0 Xa1 Dt0 Xa2 Dt1 bk0 Dt2 Xa3 bk1 Dt3 Z0 bk2 Np3 bk3 bA3 XO0 XO1 Z1 XO3 XO2",
+        "v": "gy0 gy1 w0 gy2 w1 sc0 vc0 w2 sc1 gy3 vA0 w3 sc2 omB sc3 vA1 cN2 id1 omA vA2 iw1 rs0 rs1 rs2 vf rs3",
+    },
+    "norm": {
+        "g": "blk2",
+        "s": "gx0 gx1 gx2 cm0 gx3 cA0 cN0 sa0 cm2 sa1 cm3 cA2 cN2 sa2 cA3 sa3",
+        "t": "Xa0 Xa1 Xa2 Dt0 Np0 Dt1 bk0 bA0 Xa3 Dt2 bk1 Dt3 Np2 bA2 Np3 XO0 bk2 bk3 XO1 bA3 XO3 XO2 Z0 Z1",
+        "v": "gy0 w0 gy1 vf w1 sc0 gy2 gy3 w2 sc1 vc1 w3 sc2 cN1 vA1 sc3 sb01 cN3 sb23",
+    },
+    "last": {
+        "s": "gx0 gx1 gx2 gx3 cm0 cN0 sa0 cm2 cA1 cN3 cN2 sa1 cA2 zcp sa23 fs1 fs2",
+        "t": "Xa0 Xa1 Dt0 Xa2 Xa3 Dt1 bk0 Dt2 Dt3 bk1 Np1 bA1 bk3 bk2 Z0 Np2 Z1 NA2",
+        "v": "gy0 gy1 w0 gy3 w1 sc0 gy2 w2 sc1 w3 vA0 vc1 sc2 sc3 cN1 vc3 sb01 vA3 sb23 fq0 fv1 fq3 fv2",
+        "y": "Syz Syw Syd0 Syd1",
+    },
+})
+PLAN.update({
+    "gate": 0,
+    "start": {
+        "y": "Lzo Lnd Lwt Ldl1 Lwl1 Lzr",
+        "s": "Ldr Lwl0 Ldl0 Lnw hp j9 hr vT r1 rw0 rw2 zw1 rw1",
+        "g": "pi sel eye j1 pw jm up off0",
+        "v": "ones vp1 pw0 pads zw0 pj hn vp0 icol padv hq iw0 icb om0 lx r0 id0 om1 e15 om2 vf0 om3",
+        "t": "zb0 vT0 vT1 vT2 zb1 zb2 zb3 XO0 XO1 XO2 XO3",
+    },
+    "first": {
+        "g": "blk1",
+        "s": "gx01 gx2 conv gx3 cm0 cm1 cN0 cN1 sa0 vf sa1 cA2 cN3 sa2 cA3 sa3",
+        "t": "Xa0 Xa1 Xa2 Dt0 Dt1 Dt2 bk0 Xa3 bk1 Dt3 bk2 XO1 Np2 NA2 bk3 Np3 NA3 XO0 XO3 Z0 XO2 Z1",
+        "v": "gy0 gy1 w0 gy2 w1 w2 sc0 sc1 gy3 sc2 w3 vA0 vc2 vA1 sc3 cN2 vc3 sb01 sb23",
+    },
+    "edge": {
+        "g": "sy0 sn0 sy123 sn1 sn2 sn3 off1",
+        "s": "gx0 gx1 gx2 gx3 cN0 cm1 cN1 cm2 cm3 sa0 cN3 sa1 cA3 sa23",
+        "t": "Xa0 Xa1 Dt0 Xa2 Dt1 bk0 Xa3 Dt2 bk1 Dt3 bk2 bk3 Np3 bA3 XO1 XO2 XO0 Z0 XO3 Z1",
+        "v": "gy0 gy1 w0 gy2 w1 sc0 vc0 w2 sc1 gy3 vA0 w3 sc2 omB sc3 vA1 iw1 cN2 omA vA2 rs0 id1 rs1 vf rs2 rs3",
+    },
+    "norm": {
+        "g": "blk2",
+        "s": "gx0 gx1 gx2 gx3 cm0 cN0 cN1 sa0 vf sa1 cA2 cN3 sa2 cA3 sa3",
+        "t": "Xa0 Xa1 Xa2 Dt0 Dt1 Dt2 bk0 Xa3 bk1 Dt3 bk2 Np2 Z0 NA2 bk3 Np3 bA3 XO2 XO3 XO1 Z1 XO0",
+        "v": "gy0 gy1 w0 gy2 w1 w2 sc0 gy3 sc1 vc1 sc2 w3 vA0 vc2 vA1 sc3 cN2 vc3 sb01 sb23",
+    },
+    "last": {
+        "s": "gx0 gx1 gx2 gx3 cm0 cN0 cm1 cm2 sa0 cA1 cN3 cN2 sa1 zcp sa23 fs1 fs2",
+        "t": "Xa0 Xa1 Dt0 Xa2 Dt1 Xa3 bk0 Dt2 Dt3 bk1 Np1 NA1 bk3 bk2 Z0 Z1",
+        "v": "gy0 gy1 w0 gy3 w1 sc0 gy2 w2 w3 sc1 sc2 vA0 sc3 cN1 vc3 sb01 vA2 vA3 sb23 fq0 fv1 fq3 fv2",
+        "y": "Syz Syw Syd0 Syd1",
+    },
+})
+PLAN.update({
+    "om": {}, "nz": 12,
+    "start": {
+        "y": "Ldl0 Lwl0 Lnd Lwl1 Lzc Lzq",
+        "s": "Lzo Ldr Lwt Lnw Ldl1 hp i2 hq hn r0 hr r1 vT zw1 rw0 rw1 vf0 rw2",
+        "g": "eye pi sel j1 pw up jm Lcv off0 m2i s2i",
+        "v": "ones vp1 pw0 pj vp0 icol pads zw0 id0 om0 om1 iw0 j9 e15 padv lx om2 om3",
+        "t": "zb0 zb1 zb2 vT0 vT1 vT2 zb3 XO0 XO1 XO2 XO3",
+    },
+    "first": {
+        "g": "blk1",
+        "s": "gx0 gx12 zsq gx3 cm0 cm1 vf cN0 cN1 sa0 sa1 cA2 cN3 cA3 sa23",
+        "t": "Xa0 Xa1 Xa2 Dt0 Dt1 Dt2 bk0 Xa3 bk1 Dt3 bk2 Np2 Np3 NA2 bk3 bA3 XO0 Z0 XO1 XO3 XO2 Z1",
+        "v": "gy0 gy1 w0 gy2 w1 w2 sc0 sc1 gy3 sc2 w3 vA0 vc2 vA1 sc3 cN2 vc3 sb01 sb23",
+    },
+    "edge": {
+        "g": "sy01 sn0 sn1 sy23 off1 sn23",
+        "s": "gx0 gx1 gx2 os0 gx3 os1 cN0 cm1 cN1 sa0 cN2 cN3 sa1 sa3 sa2",
+        "t": "oq0 oq1 Xa0 Xa1 Dt0 Xa2 Dt1 bk0 Xa3 Dt2 bk1 Dt3 bk2 bk3 XO2 Z0 XO0 Z1 XO3 XO1",
+        "v": "gy0 gy1 w0 gy2 w1 sc0 vc0 w2 sc1 gy3 w3 vA0 sc2 iw1 vc2 sc3 vf vc3 id1 vA1 rs0 vA3 rs1 vA2 rs23",
+    },
+    "norm": {
+        "g": "blk2",
+        "s": "gx0 gx12 gx3 os0 os1 cm0 cN0 cN1 sa0 vf sa1 cA2 cN3 sa2 cA3 sa3",
+        "t": "oq0 oq1 Xa0 Xa1 Xa2 Xa3 Dt0 Dt1 Dt2 bk0 bk1 Dt3 bk2 Np2 NA2 bk3 Np3 XO1 NA3 Z0 XO2 Z1 XO3 XO0",
+        "v": "gy0 gy1 w0 gy2 w1 w2 sc0 gy3 sc1 vc1 w3 sc2 vA0 vc2 vA1 sc3 cN2 vc3 sb01 sb23",
+    },
+})
 
 
 def build(T, topo, core, g, plan):
@@ -69,7 +200,9 @@ def build(T, topo, core, g, plan):
     dst = T.cores[(r - 1) % n]
     rid, pid = topo.addr(dst)[0], topo.addr(dst)[1]
     mask = topo.mask(core, dst)
-    neng = len(topo.engines(core, dst))
+    engines = topo.engines(core, dst)
+    neng = len(engines)
+    halves = [sum(1 << e for e in part) for part in (engines[:neng // 2], engines[neng // 2:])]
     nin = len(topo.engines(T.cores[(r + 1) % n], core))
     V, S, P = g.vector, g.scalar, g.tensor
     queues = {"y": [], "s": [], "g": [], "v": [], "t": []}
@@ -81,11 +214,16 @@ def build(T, topo, core, g, plan):
         queues.setdefault(q, []).append({"q": q, "name": name, "fn": fn, "R": R, "W": Wr, "gives": gives or [name], "needs": needs, "kind": kind})
 
     def dma(q, name, pairs, R, Wr, needs=()):
-        eng = g.sync if q == "y" else g.scalar
+        eng = {"y": g.sync, "s": g.scalar, "g": g}[q]
         add(q, name, lambda: [eng.dma_start(o, i) for o, i in pairs], R, Wr, list(needs), kind="d")
 
     def remote(name, out, in_, R, Wr, needs, gives):
         add("g", name, lambda: g.remote_dma(out, in_, T.sem["a_" + name], T.sem.sent, pid, rid, mask), R, [], needs, ["s_" + name], "r")
+        add("x" + name, name, None, [], Wr, ["s_" + name], gives, "a")
+
+    def both(outs, ins, name, R, Wr, needs, gives):
+        tr = [RemoteDMATransfer(dst_ids=[DstId(rid=rid, pnc=pid)], dma_engine_mask=halves[i], remote_sem=T.sem["a_" + name], src=ins[i], dst=outs[i]) for i in (0, 1)]
+        add("g", name, lambda: g.remote_dma_fused(tr, local_sem=T.sem.sent), R, [], needs, ["s_" + name], "r")
         add("x" + name, name, None, [], Wr, ["s_" + name], gives, "a")
 
     def asel(name, out, src, pat, op, base, cm, R, Wr):
@@ -115,19 +253,32 @@ def build(T, topo, core, g, plan):
         elif bias is None: cp(name, out, in_, R, Wr, needs, gives)
         else: ts(name, out, in_, bias, None, [ALU.add], R, Wr, needs, gives)
 
+    def times(q, name, out, in_, scale, R, Wr, needs):
+        if q == "s": add(q, name, lambda: S.activation(out, in_, AF.Identity, scale=scale), R, Wr, needs)
+        else: ts(name, out, in_, scale, None, [ALU.mult], R, Wr, needs)
+
     col = lambda k: T.cols[:, 4 * k:4 * k + 1]
     cr = lambda k: ("cols", k, k + 1)
     npre, NL, CH, UP = plan["npre"], plan["nl"], plan["ch"], plan["up"]
     NC = len(CH) - 1
-    db = lambda m, c: "D%d" % ((m * NC + c) % 3)
-    zb_bank = lambda k: "D%d" % (k % 3)
+    sums = "nb0" in plan["edge"]["v"].split()
+    ND = 7 - NC
+    db = lambda m, c: "P%d" % (NC + (m * NC + c) % ND)
+    zb_bank = lambda k: "P%d" % (NC + k % ND)
     last = lambda kk, m=M - 1: ["%s%d_%d" % (kk, m, c) for c in range(NC)]
     oms = lambda a, b: ["om%d" % k for k in range(a // 512, (b - 1) // 512 + 1)]
     lists = lambda m, k: [k + ("0" if m * 64 < NL else "1")]
 
+    CS = plan["cs"]
+
+    def freed(m, c):
+        j = m * NC + c - ND
+        if j < 0: return ["om%d" % i for i in range(npre) if zb_bank(i) == db(m, c)]
+        return ["%s%d_%d" % (("sc" if KIND[j // NC] in plan["nhi"] else "cN",) + divmod(j, NC))]
+
     def fixed(q, w, m):
-        if w == "Lzo": dma(q, "zo", [(T.zt[0:8, 0:npre * 512], T.zo[:, 0:npre * 512])], [], ["zt"])
-        elif w == "Lzr": dma(q, "zr", [(T.zr[i:128:16, npre * 512:], T.zo[:, npre * 512:]) for i in range(16)], [], ["zr"])
+        if w == "Lzo": dma(q, "zo", [(T.zt[0:8, 0:plan["nz"] * 512], T.zo[:, 0:plan["nz"] * 512])], [], ["zt"])
+        elif w == "Lzr": dma(q, "zr", [(T.zr[i:128:16, npre * 512:], T.zo[:, npre * 512:]) for i in range(16)], [("y1", 0, 1)] * plan["gate"], ["zr"], ["gy0_0"] * plan["gate"])
         elif w == "Ldr": dma(q, "dr", [(T.vt[:, :], T.dr[:, :])], [], ["vt"])
         elif w[:3] in ("Ldl", "Lwl"):
             a, b = ((0, NL), (NL, 384))[int(w[3])]
@@ -151,24 +302,28 @@ def build(T, topo, core, g, plan):
         elif w == "pw0": fill(w, T.pw[:, 0:16], 0.0, [("pw", 0, 16)])
         elif w == "vp1": fill(w, T.vp[:, :], 1.0, ["vp"])
         elif w == "vp0": fill(w, T.vp[:, 0:2 * TK:16], 0.0, ["vp"], ["vp1"])
-        elif w == "padv": fill(w, T.cv[:, :], 2.0, ["cv"])
-        elif w == "pads": fill(w, T.cs[:, :], 1.0, ["cs"])
+        elif w == "padv": fill(w, T.cv[:, 0:TK + 8 * PAD:16], 2.0, ["cv"])
+        elif w == "pads": fill(w, T.cs[:, 0:TK + 8 * PAD:16], 1.0, ["cs"])
         elif w == "pj": ts(w, T.pj[:, 0:1], T.pi[:, 0:1], 15, None, [ALU.bitwise_and], ["pi"], [w], ["pi"])
         elif w == "icol": cp(w, col(0), T.pj[:, 0:1], ["pj"], [cr(0)], ["pj"])
         elif w == "icb": cp(w, T.icb[:, 0:1], col(0), [cr(0)], [w], ["icol"])
         elif w == "e15": ts(w, col(1), col(0), 15.0, -1.0, [ALU.is_equal, ALU.add], [cr(0)], [cr(1)], ["icol"])
-        elif w == "j9": ts(w, T.t3[:, :], T.jm[:, :], -9.0, None, [ALU.mult], ["jm"], ["t3"], ["jm"])
+        elif w == "kc0": fill(w, T.kc[:, :], 0.0, ["kc"])
+        elif w == "kc": plus(q, w, T.kc[:, :], T.kc[:, :], col(1), ["kc", cr(1)], [w], ["kc0", "e15"])
+        elif w == "j9": times(q, w, T.t3[:, :], T.jm[:, :], -9.0, ["jm"], ["t3"], ["jm"])
         elif w == "lx": tt(w, T.lx[:, :], T.t3[:, :], T.eye[:, :], ALU.add, ["t3", "eye"], [w], ["j9", "eye"])
-        elif w == "r0": ts(w, T.r0[:, :], T.up[:, :], -32.0, None, [ALU.mult], ["up"], [w], ["up"])
-        elif w == "r1": cp(w, T.r0[:, 0:B:16], T.jm[:, 0:B:16], ["jm"], ["r0"], ["jm", "r0"])
-        elif w in ("hp", "hn"): ts(w, T[w][:, :], T.eye[:, :], 0.5 if w == "hp" else -0.5, None, [ALU.mult], ["eye"], [w], ["eye"])
-        elif w == "zw1": ts(w, T.zw[:, 11:96:12], T.jm[:, 0:B:16], col(0), None, [ALU.mult], ["jm", "zw", cr(0)], ["zw"], ["jm", "icol", "zw0"])
+        elif w == "r0": times(q, w, T.r0[:, :], T.up[:, :], -32.0, ["up"], [w], ["up"])
+        elif w == "r1": plus(q, w, T.r0[:, 0:B:16], T.jm[:, 0:B:16], None, ["jm"], ["r0"], ["jm", "r0"])
+        elif w == "hp" and q == "s" and plan["early"]: add(q, w, lambda: S.activation(T.hp[:, :], T.eye[:, :], AF.Silu, scale=32.0), ["eye"], [w], ["eye"])
+        elif w in ("hp", "hn"): times(q, w, T[w][:, :], T.eye[:, :], 32.0 if w == "hp" else -32.0, ["eye"], [w], ["eye"])
+        elif w in ("hq", "hr"): times(q, w, T[w][:, :], T.eye[:, :], 0.5 if w == "hq" else -0.5, ["eye"], [w], ["eye"])
+        elif w == "zw1": times(q, w, T.zw[:, 11:96:12], T.jm[:, 0:B:16], col(0), ["jm", "zw", cr(0)], ["zw"], ["jm", "icol", "zw0"])
         elif w[:2] == "rw":
             h = int(w[2])
-            ts(w, T.rw[:, h * B:(h + 1) * B], T.r0[:, :], T.wts[:, h:h + 1], None, [ALU.mult], ["r0", "wts"], [("rw", h, h + 1)], ["r1", "wt"])
+            times(q, w, T.rw[:, h * B:(h + 1) * B], T.r0[:, :], T.wts[:, h:h + 1], ["r0", "wts"], [("rw", h, h + 1)], ["r1", "wt"])
         elif w[:2] == "zb":
             k = int(w[2:]); b = zb_bank(k)
-            mm(w, [(T[b][:, 0:512], T.sel[0:8, :], T.zt[0:8, k * 512:(k + 1) * 512], True, True)], ["sel", "zt"], [b], ["sel", "zo"] + (["om%d" % (k - 3)] if k >= 3 else []))
+            mm(w, [(T[b][:, 0:512], T.sel[0:8, :], T.zt[0:8, k * 512:(k + 1) * 512], True, True)], ["sel", "zt"], [b], ["sel", "zo"] + (["om%d" % (k - ND)] if k >= ND else []))
         elif w in ("vT0", "vT1", "vT2"):
             c = int(w[2])
             mm(w, [(T.ZZ[:, 0:384], T.vt[:, c * B:(c + 1) * B], T.pw[:, 16 - 8 * c:400 - 8 * c], c == 0, c == 2)], ["vt", "pw"], ["ZZ"], ["dr", "pw", "pw0"] + (["vT%d" % (c - 1)] if c else []))
@@ -178,12 +333,31 @@ def build(T, topo, core, g, plan):
             a = (k % 2) * TK
             plus(q, "vf%d" % k, T.vp[:, a + 1:a + TK:16], T.vT[:, k * 64:(k + 1) * 64], None, ["vT"], [("vp", a, a + TK)], ["vT", "vp0"] + (last("sc", k - 2) if k >= 2 else []))
         elif w in ("omA", "omB"):
-            k = 2 * (m + 1 + "AB".index(w[2])); a = k * 512
+            k = plan["om"].get(w[2] + str(m))
+            if k is None: return True
+            a = k * TK
             ts(w, T.om[:, a:a + TK], T.zr[:, a:a + TK], T.icb[:, 0:1], None, [ALU.not_equal], ["zr", "icb"], [("om", a, a + TK)], ["zr", "icb"], oms(a, a + TK))
+        elif w == "Lzc": dma(q, "zc", [(T.zc[:, :], T.zo[:, :])], [], ["zc"])
+        elif w == "zsq": act(w, T.zc2[:, :], T.zc[:, :], AF.Square, None, ["zc"], ["zc2"], ["zc"])
+        elif w == "Lzq": dma(q, "zq", [(T.zq[0:8, :], T.zc2[:, :])], ["zc2"], ["zq"], ["zsq"])
+        elif w == "i2": act(w, col(2), col(0), AF.Square, None, [cr(0)], [cr(2)], ["icol"])
+        elif w == "m2i": add(q, w, lambda: g.iota(T.m2i[0:8, :], [[0, 8], [-2, 16]], 0, 0, allow_small_or_imprecise_dtypes=True), [], [w], [])
+        elif w == "s2i": asel(w, T.s2i[0:8, :], T.m2i[0:8, :], [[1, 8], [0, 16]], ALU.is_equal, 0, -1, ["m2i"], [w])
+        elif w in ("oq0", "oq1", "ol0", "ol1"):
+            k = 2 * (m + 1) + int(w[2]); b = db(m, 1 + int(w[2])); a = k * 512
+            free = freed(m, 1 + int(w[2])) + oms(m * TK, m * TK + TK) if w[1] == "q" else ["cN%d_%d" % (m, 1 + int(w[2]))]
+            mm("oq%d" % k, [(T[b][:, 0:512], T.s2i[0:8, :], T.zt[0:8, a:a + 512], True, False), (T[b][:, 0:512], T.sel[0:8, :], T.zq[0:8, a:a + 512], False, True)],
+               ["sel", "s2i", "zt", "zq"], [b], ["sel", "s2i", "zo", "zq"] + free)
+        elif w in ("os0", "os1"):
+            k = 2 * (m + 1) + int(w[2]); b = db(m, 1 + int(w[2])); a = k * 512
+            act("om%d" % k, T.om[:, a:a + 512], T[b][:, 0:512], AF.Sign, col(2), [b, cr(2)], [("om", a, a + 512)], ["oq%d" % k, "i2"])
+        elif w == "Lcv": dma(q, "conv", [(T.doc[:, CS:D], T.nd[:, CS:D])], [], [("doc", CS, D)], ["eye"])
+        elif w == "cvS": act(w, T.doc[:, 0:CS], T.ndb[:, 0:CS], AF.Silu, UP, ["ndb"], [("doc", 0, CS)], ["nd"])
+        elif w == "cvV": ts("conv", T.doc[:, CS:D], T.ndb[:, CS:D], UP, None, [ALU.add], ["ndb"], [("doc", CS, D)], ["nd"])
         elif w[:2] == "om":
             k = int(w[2:]); b = zb_bank(k)
             ts(w, T.om[:, k * 512:(k + 1) * 512], T[b][:, 0:512], col(0), None, [ALU.not_equal], [b, cr(0)], [("om", k * 512, (k + 1) * 512)], ["zb%d" % k, "icol"])
-        elif w == "conv": act(w, T.doc[:, :], T.ndb[:, :], AF.Silu, UP, ["ndb"], ["doc"], ["nd"])
+        elif w == "conv": act(w, T.doc[:, :], T.ndb[:, :], AF.Identity if plan["early"] else AF.Silu, None, ["ndb"], ["doc"], ["nd"])
         elif w[:3] == "off":
             h = int(w[3]); a = (2 * h + 1) * 64
             remote(w, T.nbo[:, h * 64:h * 64 + 64], T.wlu[:, a:a + 64], [("wlu", a, a + 64)], [("nbo", h, h + 1)], lists(2 * h + 1, "iw"), ["a_" + w])
@@ -195,9 +369,15 @@ def build(T, topo, core, g, plan):
             a = int(w[3]) * TK
             if q == "v": ts(w, T.ydb[:, a:a + TK], T.doc[:, a:a + TK], MAGIC - UP, MAGIC, [ALU.add, ALU.subtract], ["doc"], [("ydb", a, a + TK)], last("sa"))
             else: act(w, T.ydb[:, a:a + TK], T.doc[:, a:a + TK], AF.Relu, -UP - 2.0 ** -10, ["doc"], [("ydb", a, a + TK)], last("sa"))
+        elif w[:2] in ("fq", "fs", "fv"):
+            a = int(w[2]) * 512; y = T.ydb[:, a:a + 512]; r = [("ydb", a, a + 512)]
+            if w[1] == "q": ts(w, y, T.doc[:, a:a + 512], MAGIC, MAGIC, [ALU.add, ALU.subtract], ["doc"], r, last("sa"))
+            elif w[1] == "s": act(w, y, T.doc[:, a:a + 512], AF.Identity, OFF, ["doc"], r, last("sa"))
+            else: ts(w, y, y, -OFF, None, [ALU.add], r, r, ["fs" + w[2]], ["fq" + w[2]])
         elif w[:3] == "Syd":
             a = int(w[3]) * TK
-            dma(q, w[1:], [(T.yd[:, a:a + TK], T.ydb[:, a:a + TK])], [("ydb", a, a + TK)], [], ["fin" + w[3]])
+            dma(q, w[1:], [(T.yd[:, a:a + TK], T.ydb[:, a:a + TK])], [("ydb", a, a + TK)], [],
+                ["fin" + w[3]] if "fin0" in plan["last"]["v"] else ["fq%d" % (a // 512), "fq%d" % (a // 512 + 1)])
         elif w == "zcp": plus(q, w, T.zs[0:96, :], T.ZZ[0:96, 0:512], 120.0, ["ZZ"], ["zs"], ["Z5_1"])
         elif w == "Syz": dma(q, "yz", [(T.yz[:, :], T.zs[0:96, :])], ["zs"], [], ["zcp"])
         else: return False
@@ -208,6 +388,7 @@ def build(T, topo, core, g, plan):
         cs = [int(x) for x in w[len(k):]]
         if k == "XO": m = 0 if m == "start" else m + 1
         h = m // 2
+        CH = plan.get("ch" + KIND[m], plan["ch"])
         tag = lambda kk, cc=None, mb=m: ["%s%d_%d" % (kk, mb, c) for c in (cs if cc is None else cc)]
         c0 = cs[0]; a, b = CH[c0], CH[cs[-1] + 1]; u = b - a
         t0, t1 = m * TK + a, m * TK + b
@@ -215,7 +396,9 @@ def build(T, topo, core, g, plan):
         e0, e1 = h * TK + a, h * TK + b
         s0, s1 = (m % 2) * TK + a, (m % 2) * TK + b
         p0 = a + c0 * PAD
-        X = "X%d" % c0; Dk = db(m, c0); Wk = "W%d" % h
+        X = "P%d" % c0; Dk = db(m, c0); Wk = "W%d" % h
+        nhi = KIND[m] in plan["nhi"]
+        N, n0 = (X, 256) if nhi else (Dk, 0)
         name = "%s_%d" % (w, m)
         me = tag(k)
         blocks = range(0, u, B)
@@ -231,8 +414,7 @@ def build(T, topo, core, g, plan):
         elif k == "Xa": mm(name, [(T[X][:, 0:u], T.eye[:, :], T.ag[:, a:b], False, True)], ["eye", ("ag", a, b)], [X], tag("XO") + tag("gx"), me)
         elif k == "w": tt(name, T.wp[:, a:b], T[X][:, 0:u], T.y1[:, t0:t1], ALU.mult, [X, ("y1", t0, t1)], [("wp", a, b)], tag("Xa") + tag("gy"), me)
         elif k == "Dt":
-            j = m * NC + c0
-            prev = ["cN%d_%d" % divmod(j - 3, NC)] if j >= 3 else ["om%d" % i for i in range(npre) if zb_bank(i) == Dk]
+            prev = freed(m, c0) + (["om%d" % (2 * m + 1 + c0)] if c0 in (1, 2) and "oq0" in plan[KIND[m]]["t"] else [])
             mm(name, [(T[Dk][:, j:j + B], T.wp[:, a + j:a + j + B], T.rw[:, h * B:(h + 1) * B], True, True) for j in blocks],
                [("rw", h, h + 1), ("wp", a, b)], [Dk], tag("w") + prev + ["rw%d" % h], me)
         elif k == "sc":
@@ -242,23 +424,42 @@ def build(T, topo, core, g, plan):
         elif k == "cm": act(name, T.cs[:, p0:p0 + u], T.ee[:, a:b], AF.Sign, 0.5, [("ee", a, b)], [("cs", p0, p0 + u)], tag("sc") + ["pads"], me)
         elif k == "bk":
             c = "cv" if ("vc%d" % c0) in plan[KIND[m]]["v"].split() else "cs"
-            mm(name, [(T[Dk][:, j:j + B], T[c][:, p0 + j + i:p0 + j + i + B], T[("hp", "hn")[i]][:, :], i == 0, i == 1) for j in blocks for i in (0, 1)],
-               ["hp", "hn", (c, p0, p0 + u + PAD)], [Dk], tag("cm") + ["hp", "hn"], me)
-        elif k == "cN": plus(q, name, T.nm[:, t0:t1], T[Dk][:, 0:u], col(1), [Dk, cr(1)], [("nm", t0, t1)], tag("bk") + ["e15"], me)
+            mm(name, [(T[N][:, n0 + j:n0 + j + B], T[c][:, p0 + j + i:p0 + j + i + B], T[("hp", "hn")[i]][:, :], i == 0, i == 1) for j in blocks for i in (0, 1)],
+               ["hp", "hn", (c, p0, p0 + u + PAD)], [N], tag("cm") + ["hp", "hn"], me)
+        elif k == "cN":
+            if q == "s":
+                add(q, name, lambda: S.activation(T.nm[:, t0:t1], T[N][:, n0:n0 + u], AF.Identity, bias=col(1), scale=1.0 / 64),
+                    [N, cr(1)], [("nm", t0, t1)], tag("bk") + ["e15"], me)
+            else: ts(name, T.nm[:, t0:t1], T[N][:, n0:n0 + u], 1.0 / 64, col(1), [ALU.mult, ALU.add], [N, cr(1)], [("nm", t0, t1)], tag("bk") + ["e15"], me)
         elif k == "Np":
             mm(name, [(T[X][:, 0:u], T.lx[:, :], T.om[:, t0:t1], True, False), (T[X][:, 0:u], T.eye[:, :], T.ag[:, a:b], False, False)],
-               ["lx", "eye", ("om", t0, t1), ("ag", a, b)], [X], tag("w"), me)
+               ["lx", "eye", ("om", t0, t1), ("ag", a, b)], [X], tag("cN" if nhi else "w"), me)
         elif k == "NA": mm(name, [(T[X][:, 0:u], T.eye[:, :], T.nm[:, t0:t1], False, True)], ["eye", ("nm", t0, t1)], [X], tag("cN") + tag("Np"), me)
+        elif k == "bA":
+            c = "cv" if ("vc%d" % c0) in plan[KIND[m]]["v"].split() else "cs"
+            mm(name, [(T[X][:, j:j + B], T[c][:, p0 + j + i:p0 + j + i + B], T[("hq", "hr")[i]][:, :], False, i == 1 and j + B == u) for j in blocks for i in (0, 1)],
+               ["hq", "hr", (c, p0, p0 + u + PAD)], [X], tag("cm") + tag("Np") + ["hq", "hr"], tag("NA"))
+        elif k == "cA" and ("bA%d" % c0) in plan[KIND[m]]["t"].split():
+            plus(q, name + "b", T.na[:, a:b], T[X][:, 0:u], col(1), [X, cr(1)], [("na", a, b)], tag("NA"), me)
         elif k == "cA": plus(q, name, T.na[:, a:b], T[X][:, 0:u], UP, [X], [("na", a, b)], tag("NA"), me)
         elif k == "vA": tt(name, T.na[:, a:b], T[X][:, 0:u], T.nm[:, t0:t1], ALU.add, [X, ("nm", t0, t1)], [("na", a, b)], tag("cN"), tag("cA"))
         elif k == "sa":
             act(name, T.doc[:, 0:D].indirect(T.dlu[:, o0:o1]), T.na[:, a:b], AF.Silu, None, [("na", a, b), ("dlu", o0, o1)], ["doc"],
-                tag("cA") + ["conv"], me)
+                tag("cA") + ["conv"] + (["cvS"] if CS else []), me)
         elif k == "sb":
             tt(name, wordw(), T.y1[:, t0:t1], T.nm[:, t0:t1], ALU.add, [("y1", t0, t1), ("nm", t0, t1), ("wlu", o0, o1)], [Wk], tag("cN"), me)
         elif k in ("sy", "sn"):
             src, land = (("y1", "yrecv"), ("nm", "nrecv"))[k == "sn"]
             remote("%s%d_%d" % (k[1], h, c0), T[land][:, e0:e1], T[src][:, t0:t1], [(src, t0, t1)], [(land, e0, e1)], tag("gy" if k == "sy" else "cN"), tag("a" + k))
+        elif k == "sf":
+            both((T.yrecv[:, e0:e1], T.nrecv[:, e0:e1]), (T.y1[:, t0:t1], T.nm[:, t0:t1]), "n%d_%d" % (h, c0), [("y1", t0, t1), ("nm", t0, t1)],
+                 [("yrecv", e0, e1), ("nrecv", e0, e1)], tag("cN"), tag("asy") + tag("asn"))
+        elif k == "nb": tt(name, T.nsend[:, e0:e1], T[N][:, n0:n0 + u], T.y1[:, t0:t1], ALU.add, [N, ("y1", t0, t1)], [("nsend", e0, e1)], tag("bk"), me)
+        elif k == "sd": remote("n%d_%d" % (h, c0), T.nrecv[:, e0:e1], T.nsend[:, e0:e1], [("nsend", e0, e1)], [("nrecv", e0, e1)], tag("nb"), tag("asn"))
+        elif k == "rs" and sums:
+            Wn = "W%d" % (h + 1)
+            tt(name, T[Wn][:, 0:W].indirect(T.nbo[:, h * 64 + a // 16:h * 64 + b // 16]), T.nrecv[:, e0:e1], T.kc[:, 0:u], ALU.add,
+               [("nrecv", e0, e1), "kc", ("nbo", h, h + 1)], [Wn], tag("asn") + ["kc", "a_off%d" % h, "a_blk%d" % (h + 1)], tag("sb"))
         elif k == "rs":
             Wn = "W%d" % (h + 1)
             tt(name, T[Wn][:, 0:W].indirect(T.nbo[:, h * 64 + a // 16:h * 64 + b // 16]), T.yrecv[:, e0:e1], T.nrecv[:, e0:e1], ALU.add,
@@ -274,7 +475,7 @@ def build(T, topo, core, g, plan):
     for m in ["start"] + list(range(M)):
         for q in "ysvtg":
             for w in plan[m if m == "start" else KIND[m]].get(q, "").split():
-                if ONLY.get(w, m) == m and not fixed(q, w, m): chunk(q, m, w)
+                if m in ("start", ONLY.get(w, m)) and not fixed(q, w, m): chunk(q, m, w)
 
     order, have, pos = [], set(), {q: 0 for q in queues}
     moved = True
@@ -321,8 +522,9 @@ def emit(order, neng, nin, g, T):
                     if kn.get(s, 0) < v: kn[s] = v
             ins = o["fn"]()
             if o["kind"] == "c":
-                count[q] += 1
-                ins.then_inc(T.sem["c" + q], 1)
+                for i in (ins if isinstance(ins, list) else [ins]):
+                    count[q] += 1
+                    i.then_inc(T.sem["c" + q], 1)
                 o["sig"] = ("c" + q, count[q])
             elif o["kind"] == "d":
                 for i in ins:

from concourse.bass import DstId, RemoteDMATransfer
from concourse.mybir import AluOpType as ALU, ActivationFunctionType as AF

D, W, H, TK, M = 2048, 4096, 3, 1024, 6
B = 128
PAD = 16
OFF = 135.0
MAGIC = 12582912.0

SCRATCH = {}
for _n, _c in (("W0", W), ("W1", W), ("W2", W), ("ndb", D), ("ydb", D), ("zt", M * TK), ("om", M * TK), ("zr", M * TK),
               ("y1", M * TK), ("nm", M * TK), ("yrecv", 2 * TK), ("nrecv", 2 * TK), ("ag", TK), ("vp", 2 * TK), ("nsend", 2 * TK), ("kc", TK),
               ("zc", 384), ("zc2", 384), ("zq", M * TK), ("m2i", B), ("s2i", B),
               ("ee", TK), ("cv", TK + 8 * PAD), ("cs", TK + 8 * PAD), ("zs", 512), ("zw", 112), ("vt", 384), ("vT", 384), ("pw", 400),
               ("ones", 384), ("sel", B), ("j1", B), ("jm", B), ("eye", B), ("up", B), ("lx", B), ("hp", B), ("hn", B), ("hq", B), ("hr", B),
               ("r0", B), ("t3", B), ("icb", 8)):
    SCRATCH[_n] = ("sbuf", [128, _c], "bfloat16")
for _n, _c in (("doc", D), ("wts", 4), ("wp", TK), ("na", TK), ("rw", 384), ("cols", 16)):
    SCRATCH[_n] = ("sbuf", [128, _c], "float32")
for _n, _c, _t in (("dli", 384, "int32"), ("wli", 384, "int32"), ("pi", 4, "int32"), ("pj", 4, "int32"),
                   ("dlu", 384, "uint16"), ("wlu", 384, "uint16"), ("nbo", 128, "uint16")):
    SCRATCH[_n] = ("sbuf", [128, _c], _t)
BANKS = ("P0", "P1", "P2", "P3", "P4", "P5", "P6", "ZZ")
for _n in BANKS:
    SCRATCH[_n] = ("psum", [128, 512], "float32")
DMAS = ["conv", "zc", "zq", "zo", "dl0", "wl0", "dr", "wt", "nd", "nw", "dl1", "wl1", "zr", "yw", "yd0", "yd1", "yz"]
ARRS = ["off0", "off1", "blk1", "blk2"] + ["%s%d_%d" % (k, s, c) for k in "yn" for s in (0, 1) for c in range(5)]
SEMAPHORES = ["cv", "cs", "ct", "cg", "sent"] + ["d_" + n for n in DMAS] + ["a_" + n for n in ARRS]

KIND = ["first", "edge", "norm", "edge", "norm", "last"]
ONLY = {"id1": 1, "iw1": 1, "off1": 1, "blk2": 2}
PLAN = {
    "om": {"A1": 2, "B1": 3, "A3": 4, "B3": 5},
    "gate": 1, "early": 1, "cs": 0, "nz": 4, "nhi": (), "up": 0.0, "npre": 4, "nl": 128, "ch": [0, 256, 512, 768, 1024],
    "start": {
        "y": "Lzo Ldr Lnd Lnw Lwl1 Ldl1 Lzr",
        "s": "Ldl0 Lwl0 Lwt",
        "g": "pi sel j1 jm eye pw up off0",
        "v": "ones vp1 pj zw0 pw0 vp0 padv pads icol e15 icb om0 id0 iw0 j9 lx om1 hp hn r0 r1 zw1 om2 vT vf0 om3 rw0 rw1 rw2",
        "t": "zb0 zb1 zb2 vT0 vT1 vT2 XO0 zb3 XO1 XO2 XO3",
    },
    "first": {
        "g": "blk1",
        "s": "gx012 gx3 vf conv cm0 cm1 cN0 cN1 sa0 sa1 cN2 cN3 cA2 sa23",
        "t": "Xa0 Xa1 Xa2 Xa3 Dt0 Dt1 Dt2 bk0 bk1 Dt3 Np2 bk2 bk3 NA2 Z0 XO0 XO1 XO2 Z1 XO3",
        "v": "gy0 gy1 w0 w1 gy2 w2 sc0 sc1 gy3 w3 sc2 vA0 vA1 vc2 sc3 vc3 sb01 vA3 sb23",
    },
    "edge": {
        "g": "sy0123 sn0 sn1 sn23 off1",
        "s": "gx0 vf gx1 gx2 gx3 cN0 cm1 cm2 cN1 cN2 cN3 sa0 sa123",
        "t": "Xa0 Xa1 Dt0 Xa2 Xa3 Dt1 bk0 Dt2 Dt3 bk1 bk2 bk3 Z0 Z1 XO0 XO1 XO2 XO3",
        "v": "gy01 gy2 w0 gy3 w1 sc0 vc0 w2 w3 sc1 omA sc2 vA0 sc3 vc3 omB iw1 vA1 vA2 id1 vA3 rs0 rs1 rs23",
    },
    "norm": {
        "g": "blk2",
        "s": "gx0 gx12 gx3 vf cm0 cm1 cN0 cN1 cm2 sa0 cN2 sa1 cN3 cA2 cA3 sa23",
        "t": "Xa0 Xa1 Xa2 Xa3 Dt0 Dt1 Dt2 bk0 bk1 Dt3 bk2 Np3 bk3 Np2 NA2 XO0 NA3 Z0 XO1 XO2 XO3 Z1",
        "v": "gy0 gy1 w0 w1 gy2 w2 sc0 sc1 gy3 w3 sc2 vA0 vA1 sc3 vc3 sb01 sb2 sb3",
    },
    "last": {
        "s": "gx0 gx1 gx2 gx3 cN0 cm1 sa0 cN1 cN2 cm3 sa1 cN3 cA3 sa3 sa2 zcp",
        "t": "Xa0 Xa1 Dt0 Xa2 Dt1 Xa3 bk0 Dt2 Dt3 bk1 bk2 Z0 Np3 bk3 NA3 Z1",
        "v": "gy01 gy2 w0 w1 gy3 sc0 vc0 w2 sc1 w3 vA0 sc2 vc2 sb0 sc3 vA1 sb12 sb3 vA2 fin0 fin1",
        "y": "Syw Syz Syd0 Syd1",
    },
}
PLAN.update({
    "start": {
        "y": "Ldr Lzo Lnd Lnw Lwl1 Ldl1 Lzr",
        "s": "Lwl0 Lwt Ldl0 r0 r1 j9 rw0 rw2 hn vT zw1 hp rw1 vf0",
        "g": "pi j1 pw up jm sel eye off0",
        "v": "ones pads vp1 zw0 iw0 pw0 pj icol padv vp0 icb om0 lx id0 e15 om1 om2 om3",
        "t": "vT0 vT1 zb0 vT2 zb1 zb2 XO1 zb3 XO0 XO3 XO2",
    },
    "first": {
        "g": "blk1",
        "s": "gx0123 conv cm1 cN0 cN1 sa0 cN2 sa1 cN3 cA2 sa2 sa3",
        "t": "Xa2 Xa1 Xa0 Xa3 Dt0 Dt1 Np2 bk0 Dt2 bk1 Dt3 XO0 bk2 Z0 bk3 XO1 NA2 XO3 XO2 Z1",
        "v": "gy0 gy2 w0 gy1 w1 sc0 w2 vc0 sc1 gy3 vf w3 sc2 vA0 vc2 vA1 sc3 vc3 sb01 vA3 sb23",
    },
    "edge": {
        "g": "sf0 sf1 off1 sf2 sf3",
        "s": "vf gx0 gx1 gx2 gx3 cm0 cN0 cN1 sa0 cA1 cN3 sa1 cA3 sa2 sa3",
        "t": "Xa0 Xa1 Dt0 Xa2 Dt1 Xa3 bk0 Dt2 bk1 Dt3 Np1 bk2 Np3 NA1 bk3 XO0 NA3 Z0 XO3 XO2 XO1 Z1",
        "v": "gy0 gy1 w0 gy2 w1 sc0 w2 gy3 sc1 w3 vc1 omB sc2 vA0 vc2 sc3 iw1 vc3 cN2 id1 omA vA2 rs0 rs1 rs2 rs3",
    },
    "norm": {
        "g": "blk2",
        "s": "gx0 gx123 cm0 cN0 cN1 sa0 sa1 cA2 cN3 sa2 cA3 sa3",
        "t": "Xa0 Xa3 Xa2 Xa1 Dt0 Dt1 Dt2 bk0 bk1 Dt3 bk2 Np3 Np2 NA2 bk3 Z0 NA3 XO2 Z1 XO0 XO3 XO1",
        "v": "vf gy0 gy1 w0 gy2 w1 w2 sc0 gy3 sc1 vc1 w3 sc2 vA0 vc2 vA1 sc3 cN2 vc3 sb01 sb23",
    },
    "last": {
        "s": "gx0 gx1 gx23 cm0 cN0 cm1 sa0 cN2 cA1 cN3 sa1 cA3 cA2 sa23 zcp",
        "t": "Xa0 Xa1 Dt0 Xa3 Xa2 Dt1 bk0 Dt2 Dt3 bk1 Np1 bk2 Np2 NA1 bk3 Np3 Z0 NA3 Z1 NA2",
        "v": "gy0 gy1 w0 gy3 w1 sc0 gy2 w2 w3 sc1 vA0 sc2 vc2 sc3 cN1 vc3 sb01 sb23 fin0 fin1",
        "y": "Syw Syz Syd0 Syd1",
    },
})
PLAN.update({
    "start": {
        "y": "Lzo Ldr Lnd Lnw Lwl1 Ldl1 Lzr",
        "s": "Lwt Lwl0 Ldl0 hp hq hn j9 hr vT r0 vf0 r1 rw0 rw1 rw2 zw1",
        "g": "pi sel eye j1 pw jm up off0",
        "v": "ones pads pj vp1 icol padv e15 pw0 vp0 zw0 icb om0 id0 lx om1 iw0 om2 om3",
        "t": "zb0 zb1 zb2 vT0 vT1 vT2 zb3 XO0 XO1 XO2 XO3",
    },
    "first": {
        "g": "blk1",
        "s": "gx0 gx12 conv gx3 cA0 cN0 sa0 cm2 sa1 cm3 cA2 cN2 sa2 cA3 sa3",
        "t": "Xa0 Xa1 Xa2 Dt0 Np0 Dt1 bk0 bA0 Xa3 Dt2 bk1 Dt3 Np2 XO1 Np3 bA2 bk2 bk3 XO2 bA3 Z0 XO3 XO0 Z1",
        "v": "gy0 w0 gy1 vf w1 sc0 gy3 vc0 gy2 w2 sc1 vc1 w3 sc2 cN1 vA1 sc3 sb01 cN3 sb23",
    },
    "edge": {
        "g": "sy012 sn0 sy3 sn1 sn2 sn3 off1",
        "s": "gx0 gx1 gx2 gx3 cN0 cm1 cN1 cm2 cm3 sa0 cN3 cA3 sa123",
        "t": "Xa0 Xa1 Dt0 Xa2 Dt1 bk0 Dt2 Xa3 bk1 Dt3 Z0 bk2 Np3 bk3 bA3 XO0 XO1 Z1 XO3 XO2",
        "v": "gy0 gy1 w0 gy2 w1 sc0 vc0 w2 sc1 gy3 vA0 w3 sc2 omB sc3 vA1 cN2 id1 omA vA2 iw1 rs0 rs1 rs2 vf rs3",
    },
    "norm": {
        "g": "blk2",
        "s": "gx0 gx1 gx2 cm0 gx3 cA0 cN0 sa0 cm2 sa1 cm3 cA2 cN2 sa2 cA3 sa3",
        "t": "Xa0 Xa1 Xa2 Dt0 Np0 Dt1 bk0 bA0 Xa3 Dt2 bk1 Dt3 Np2 bA2 Np3 XO0 bk2 bk3 XO1 bA3 XO3 XO2 Z0 Z1",
        "v": "gy0 w0 gy1 vf w1 sc0 gy2 gy3 w2 sc1 vc1 w3 sc2 cN1 vA1 sc3 sb01 cN3 sb23",
    },
    "last": {
        "s": "gx0 gx1 gx2 gx3 cm0 cN0 sa0 cm2 cA1 cN3 cN2 sa1 cA2 zcp sa23 fs1 fs2",
        "t": "Xa0 Xa1 Dt0 Xa2 Xa3 Dt1 bk0 Dt2 Dt3 bk1 Np1 bA1 bk3 bk2 Z0 Np2 Z1 NA2",
        "v": "gy0 gy1 w0 gy3 w1 sc0 gy2 w2 sc1 w3 vA0 vc1 sc2 sc3 cN1 vc3 sb01 vA3 sb23 fq0 fv1 fq3 fv2",
        "y": "Syz Syw Syd0 Syd1",
    },
})
PLAN.update({
    "gate": 0,
    "start": {
        "y": "Lzo Lnd Lwt Ldl1 Lwl1 Lzr",
        "s": "Ldr Lwl0 Ldl0 Lnw hp j9 hr vT r1 rw0 rw2 zw1 rw1",
        "g": "pi sel eye j1 pw jm up off0",
        "v": "ones vp1 pw0 pads zw0 pj hn vp0 icol padv hq iw0 icb om0 lx r0 id0 om1 e15 om2 vf0 om3",
        "t": "zb0 vT0 vT1 vT2 zb1 zb2 zb3 XO0 XO1 XO2 XO3",
    },
    "first": {
        "g": "blk1",
        "s": "gx01 gx2 conv gx3 cm0 cm1 cN0 cN1 sa0 vf sa1 cA2 cN3 sa2 cA3 sa3",
        "t": "Xa0 Xa1 Xa2 Dt0 Dt1 Dt2 bk0 Xa3 bk1 Dt3 bk2 XO1 Np2 NA2 bk3 Np3 NA3 XO0 XO3 Z0 XO2 Z1",
        "v": "gy0 gy1 w0 gy2 w1 w2 sc0 sc1 gy3 sc2 w3 vA0 vc2 vA1 sc3 cN2 vc3 sb01 sb23",
    },
    "edge": {
        "g": "sy0 sn0 sy123 sn1 sn2 sn3 off1",
        "s": "gx0 gx1 gx2 gx3 cN0 cm1 cN1 cm2 cm3 sa0 cN3 sa1 cA3 sa23",
        "t": "Xa0 Xa1 Dt0 Xa2 Dt1 bk0 Xa3 Dt2 bk1 Dt3 bk2 bk3 Np3 bA3 XO1 XO2 XO0 Z0 XO3 Z1",
        "v": "gy0 gy1 w0 gy2 w1 sc0 vc0 w2 sc1 gy3 vA0 w3 sc2 omB sc3 vA1 iw1 cN2 omA vA2 rs0 id1 rs1 vf rs2 rs3",
    },
    "norm": {
        "g": "blk2",
        "s": "gx0 gx1 gx2 gx3 cm0 cN0 cN1 sa0 vf sa1 cA2 cN3 sa2 cA3 sa3",
        "t": "Xa0 Xa1 Xa2 Dt0 Dt1 Dt2 bk0 Xa3 bk1 Dt3 bk2 Np2 Z0 NA2 bk3 Np3 bA3 XO2 XO3 XO1 Z1 XO0",
        "v": "gy0 gy1 w0 gy2 w1 w2 sc0 gy3 sc1 vc1 sc2 w3 vA0 vc2 vA1 sc3 cN2 vc3 sb01 sb23",
    },
    "last": {
        "s": "gx0 gx1 gx2 gx3 cm0 cN0 cm1 cm2 sa0 cA1 cN3 cN2 sa1 zcp sa23 fs1 fs2",
        "t": "Xa0 Xa1 Dt0 Xa2 Dt1 Xa3 bk0 Dt2 Dt3 bk1 Np1 NA1 bk3 bk2 Z0 Z1",
        "v": "gy0 gy1 w0 gy3 w1 sc0 gy2 w2 w3 sc1 sc2 vA0 sc3 cN1 vc3 sb01 vA2 vA3 sb23 fq0 fv1 fq3 fv2",
        "y": "Syz Syw Syd0 Syd1",
    },
})
PLAN.update({
    "om": {}, "nz": 12,
    "start": {
        "y": "Ldl0 Lwl0 Lnd Lwl1 Lzc Lzq",
        "s": "Lzo Ldr Lwt Lnw Ldl1 hp i2 hq hn r0 hr r1 vT zw1 rw0 rw1 vf0 rw2",
        "g": "eye pi sel j1 pw up jm Lcv off0 m2i s2i",
        "v": "ones vp1 pw0 pj vp0 icol pads zw0 id0 om0 om1 iw0 j9 e15 padv lx om2 om3",
        "t": "zb0 zb1 zb2 vT0 vT1 vT2 zb3 XO0 XO1 XO2 XO3",
    },
    "first": {
        "g": "blk1",
        "s": "gx0 gx12 zsq gx3 cm0 cm1 vf cN0 cN1 sa0 sa1 cA2 cN3 cA3 sa23",
        "t": "Xa0 Xa1 Xa2 Dt0 Dt1 Dt2 bk0 Xa3 bk1 Dt3 bk2 Np2 Np3 NA2 bk3 bA3 XO0 Z0 XO1 XO3 XO2 Z1",
        "v": "gy0 gy1 w0 gy2 w1 w2 sc0 sc1 gy3 sc2 w3 vA0 vc2 vA1 sc3 cN2 vc3 sb01 sb23",
    },
    "edge": {
        "g": "sy01 sn0 sn1 sy23 off1 sn23",
        "s": "gx0 gx1 gx2 os0 gx3 os1 cN0 cm1 cN1 sa0 cN2 cN3 sa1 sa3 sa2",
        "t": "oq0 oq1 Xa0 Xa1 Dt0 Xa2 Dt1 bk0 Xa3 Dt2 bk1 Dt3 bk2 bk3 XO2 Z0 XO0 Z1 XO3 XO1",
        "v": "gy0 gy1 w0 gy2 w1 sc0 vc0 w2 sc1 gy3 w3 vA0 sc2 iw1 vc2 sc3 vf vc3 id1 vA1 rs0 vA3 rs1 vA2 rs23",
    },
    "norm": {
        "g": "blk2",
        "s": "gx0 gx12 gx3 os0 os1 cm0 cN0 cN1 sa0 vf sa1 cA2 cN3 sa2 cA3 sa3",
        "t": "oq0 oq1 Xa0 Xa1 Xa2 Xa3 Dt0 Dt1 Dt2 bk0 bk1 Dt3 bk2 Np2 NA2 bk3 Np3 XO1 NA3 Z0 XO2 Z1 XO3 XO0",
        "v": "gy0 gy1 w0 gy2 w1 w2 sc0 gy3 sc1 vc1 w3 sc2 vA0 vc2 vA1 sc3 cN2 vc3 sb01 sb23",
    },
})


def build(T, topo, core, g, plan):
    n = len(T.cores)
    r = T.rank_of(core)
    dst = T.cores[(r - 1) % n]
    rid, pid = topo.addr(dst)[0], topo.addr(dst)[1]
    mask = topo.mask(core, dst)
    engines = topo.engines(core, dst)
    neng = len(engines)
    halves = [sum(1 << e for e in part) for part in (engines[:neng // 2], engines[neng // 2:])]
    nin = len(topo.engines(T.cores[(r + 1) % n], core))
    V, S, P = g.vector, g.scalar, g.tensor
    queues = {"y": [], "s": [], "g": [], "v": [], "t": []}
    full = lambda b: (b, 0, 1 << 20)

    def add(q, name, fn, R, Wr, needs, gives=None, kind="c"):
        R = [full(x) if isinstance(x, str) else x for x in R]
        Wr = [full(x) if isinstance(x, str) else x for x in Wr]
        queues.setdefault(q, []).append({"q": q, "name": name, "fn": fn, "R": R, "W": Wr, "gives": gives or [name], "needs": needs, "kind": kind})

    def dma(q, name, pairs, R, Wr, needs=()):
        eng = {"y": g.sync, "s": g.scalar, "g": g}[q]
        add(q, name, lambda: [eng.dma_start(o, i) for o, i in pairs], R, Wr, list(needs), kind="d")

    def remote(name, out, in_, R, Wr, needs, gives):
        add("g", name, lambda: g.remote_dma(out, in_, T.sem["a_" + name], T.sem.sent, pid, rid, mask), R, [], needs, ["s_" + name], "r")
        add("x" + name, name, None, [], Wr, ["s_" + name], gives, "a")

    def both(outs, ins, name, R, Wr, needs, gives):
        tr = [RemoteDMATransfer(dst_ids=[DstId(rid=rid, pnc=pid)], dma_engine_mask=halves[i], remote_sem=T.sem["a_" + name], src=ins[i], dst=outs[i]) for i in (0, 1)]
        add("g", name, lambda: g.remote_dma_fused(tr, local_sem=T.sem.sent), R, [], needs, ["s_" + name], "r")
        add("x" + name, name, None, [], Wr, ["s_" + name], gives, "a")

    def asel(name, out, src, pat, op, base, cm, R, Wr):
        add("g", name, lambda: g.affine_select(out, src, pat, op, 0.0, base, cm), R, Wr, R)

    def fill(name, out, x, Wr, needs=()):
        add("v", name, lambda: V.memset(out, x), [], Wr, list(needs))

    def ts(name, out, in0, s1, s2, ops, R, Wr, needs, gives=None):
        add("v", name, lambda: V.tensor_scalar(out, in0, s1, s2, *ops), R, Wr, needs, gives)

    def tt(name, out, in0, in1, op, R, Wr, needs, gives=None):
        add("v", name, lambda: V.tensor_tensor(out, in0, in1, op), R, Wr, needs, gives)

    def cp(name, out, in_, R, Wr, needs, gives=None):
        add("v", name, lambda: V.tensor_copy(out, in_), R, Wr, needs, gives)

    def mm(name, calls, R, Wr, needs, gives=None):
        add("t", name, lambda: [P.matmul(*c) for c in calls][-1], R, Wr, needs, gives)

    def act(name, out, in_, f, bias, R, Wr, needs, gives=None):
        if bias is None: add("s", name, lambda: S.activation(out, in_, f), R, Wr, needs, gives)
        else: add("s", name, lambda: S.activation(out, in_, f, bias=bias), R, Wr, needs, gives)

    def plus(q, name, out, in_, bias, R, Wr, needs, gives=None):
        if q == "s": act(name, out, in_, AF.Identity, bias, R, Wr, needs, gives)
        elif bias is None: cp(name, out, in_, R, Wr, needs, gives)
        else: ts(name, out, in_, bias, None, [ALU.add], R, Wr, needs, gives)

    def times(q, name, out, in_, scale, R, Wr, needs):
        if q == "s": add(q, name, lambda: S.activation(out, in_, AF.Identity, scale=scale), R, Wr, needs)
        else: ts(name, out, in_, scale, None, [ALU.mult], R, Wr, needs)

    col = lambda k: T.cols[:, 4 * k:4 * k + 1]
    cr = lambda k: ("cols", k, k + 1)
    npre, NL, CH, UP = plan["npre"], plan["nl"], plan["ch"], plan["up"]
    NC = len(CH) - 1
    sums = "nb0" in plan["edge"]["v"].split()
    ND = 7 - NC
    db = lambda m, c: "P%d" % (NC + (m * NC + c) % ND)
    zb_bank = lambda k: "P%d" % (NC + k % ND)
    last = lambda kk, m=M - 1: ["%s%d_%d" % (kk, m, c) for c in range(NC)]
    oms = lambda a, b: ["om%d" % k for k in range(a // 512, (b - 1) // 512 + 1)]
    lists = lambda m, k: [k + ("0" if m * 64 < NL else "1")]

    CS = plan["cs"]

    def freed(m, c):
        j = m * NC + c - ND
        if j < 0: return ["om%d" % i for i in range(npre) if zb_bank(i) == db(m, c)]
        return ["%s%d_%d" % (("sc" if KIND[j // NC] in plan["nhi"] else "cN",) + divmod(j, NC))]

    def fixed(q, w, m):
        if w == "Lzo": dma(q, "zo", [(T.zt[0:8, 0:plan["nz"] * 512], T.zo[:, 0:plan["nz"] * 512])], [], ["zt"])
        elif w == "Lzr": dma(q, "zr", [(T.zr[i:128:16, npre * 512:], T.zo[:, npre * 512:]) for i in range(16)], [("y1", 0, 1)] * plan["gate"], ["zr"], ["gy0_0"] * plan["gate"])
        elif w == "Ldr": dma(q, "dr", [(T.vt[:, :], T.dr[:, :])], [], ["vt"])
        elif w[:3] in ("Ldl", "Lwl"):
            a, b = ((0, NL), (NL, 384))[int(w[3])]
            dma(q, w[1:], [(T[w[1:3] + "i"][:, a:b], T[w[1:3]][:, a:b])], [], [(w[1:3] + "i", a, b)])
        elif w[:2] in ("id", "iw"):
            a, b = ((0, NL), (NL, 384))[int(w[2])]
            k = w[1] + "l"
            cp(w, T[k + "u"][:, a:b], T[k + "i"][:, a:b], [(k + "i", a, b)], [(k + "u", a, b)], [k + w[2]])
        elif w == "Lwt": dma(q, "wt", [(T.wts[:, 0:3], T.wt[:, :])], [], ["wts"])
        elif w == "Lnd": dma(q, "nd", [(T.ndb[:, :], T.nd[:, :])], [], ["ndb"])
        elif w == "Lnw": dma(q, "nw", [(T.W0[:, :], T.nw[:, :])], [], ["W0"])
        elif w == "pi": add(q, w, lambda: g.iota(T.pi[:, 0:1], [[0, 1]], 0, 1), [], [w], [])
        elif w == "sel": asel(w, T.sel[0:8, :], T.ones[0:8, 0:B], [[1, 8], [0, 16]], ALU.is_equal, 0, -1, ["ones"], [w])
        elif w == "j1": asel(w, T.j1[:, :], T.ones[:, 0:B], [[-16, 8], [0, 16]], ALU.is_ge, 0, 1, ["ones"], [w])
        elif w == "jm": asel(w, T.jm[:, :], T.j1[:, :], [[16, 8], [0, 16]], ALU.is_ge, 15, -1, ["j1"], [w])
        elif w == "eye": asel(w, T.eye[:, :], T.ones[:, 0:B], [[1, B]], ALU.is_equal, 0, -1, ["ones"], [w])
        elif w == "up": asel(w, T.up[:, :], T.j1[:, :], [[1, B]], ALU.is_equal, -1, -1, ["j1"], [w])
        elif w == "pw": asel(w, T.pw[:, 16:400], T.ones[:, :], [[1, 16], [1000, 3], [16, 8]], ALU.is_equal, 0, -1, ["ones"], [("pw", 16, 400)])
        elif w == "ones": fill(w, T.ones[:, :], 1.0, [w])
        elif w == "zw0": fill(w, T.zw[:, :], 0.0, ["zw"])
        elif w == "pw0": fill(w, T.pw[:, 0:16], 0.0, [("pw", 0, 16)])
        elif w == "vp1": fill(w, T.vp[:, :], 1.0, ["vp"])
        elif w == "vp0": fill(w, T.vp[:, 0:2 * TK:16], 0.0, ["vp"], ["vp1"])
        elif w == "padv": fill(w, T.cv[:, 0:TK + 8 * PAD:16], 2.0, ["cv"])
        elif w == "pads": fill(w, T.cs[:, 0:TK + 8 * PAD:16], 1.0, ["cs"])
        elif w == "pj": ts(w, T.pj[:, 0:1], T.pi[:, 0:1], 15, None, [ALU.bitwise_and], ["pi"], [w], ["pi"])
        elif w == "icol": cp(w, col(0), T.pj[:, 0:1], ["pj"], [cr(0)], ["pj"])
        elif w == "icb": cp(w, T.icb[:, 0:1], col(0), [cr(0)], [w], ["icol"])
        elif w == "e15": ts(w, col(1), col(0), 15.0, -1.0, [ALU.is_equal, ALU.add], [cr(0)], [cr(1)], ["icol"])
        elif w == "kc0": fill(w, T.kc[:, :], 0.0, ["kc"])
        elif w == "kc": plus(q, w, T.kc[:, :], T.kc[:, :], col(1), ["kc", cr(1)], [w], ["kc0", "e15"])
        elif w == "j9": times(q, w, T.t3[:, :], T.jm[:, :], -9.0, ["jm"], ["t3"], ["jm"])
        elif w == "lx": tt(w, T.lx[:, :], T.t3[:, :], T.eye[:, :], ALU.add, ["t3", "eye"], [w], ["j9", "eye"])
        elif w == "r0": times(q, w, T.r0[:, :], T.up[:, :], -32.0, ["up"], [w], ["up"])
        elif w == "r1": plus(q, w, T.r0[:, 0:B:16], T.jm[:, 0:B:16], None, ["jm"], ["r0"], ["jm", "r0"])
        elif w == "hp" and q == "s" and plan["early"]: add(q, w, lambda: S.activation(T.hp[:, :], T.eye[:, :], AF.Silu, scale=32.0), ["eye"], [w], ["eye"])
        elif w in ("hp", "hn"): times(q, w, T[w][:, :], T.eye[:, :], 32.0 if w == "hp" else -32.0, ["eye"], [w], ["eye"])
        elif w in ("hq", "hr"): times(q, w, T[w][:, :], T.eye[:, :], 0.5 if w == "hq" else -0.5, ["eye"], [w], ["eye"])
        elif w == "zw1": times(q, w, T.zw[:, 11:96:12], T.jm[:, 0:B:16], col(0), ["jm", "zw", cr(0)], ["zw"], ["jm", "icol", "zw0"])
        elif w[:2] == "rw":
            h = int(w[2])
            times(q, w, T.rw[:, h * B:(h + 1) * B], T.r0[:, :], T.wts[:, h:h + 1], ["r0", "wts"], [("rw", h, h + 1)], ["r1", "wt"])
        elif w[:2] == "zb":
            k = int(w[2:]); b = zb_bank(k)
            mm(w, [(T[b][:, 0:512], T.sel[0:8, :], T.zt[0:8, k * 512:(k + 1) * 512], True, True)], ["sel", "zt"], [b], ["sel", "zo"] + (["om%d" % (k - ND)] if k >= ND else []))
        elif w in ("vT0", "vT1", "vT2"):
            c = int(w[2])
            mm(w, [(T.ZZ[:, 0:384], T.vt[:, c * B:(c + 1) * B], T.pw[:, 16 - 8 * c:400 - 8 * c], c == 0, c == 2)], ["vt", "pw"], ["ZZ"], ["dr", "pw", "pw0"] + (["vT%d" % (c - 1)] if c else []))
        elif w == "vT": plus(q, w, T.vT[:, :], T.ZZ[:, 0:384], None, ["ZZ"], [w], ["vT2"])
        elif w[:2] == "vf":
            k = int(w[2:]) if w[2:] else m + 1
            a = (k % 2) * TK
            plus(q, "vf%d" % k, T.vp[:, a + 1:a + TK:16], T.vT[:, k * 64:(k + 1) * 64], None, ["vT"], [("vp", a, a + TK)], ["vT", "vp0"] + (last("sc", k - 2) if k >= 2 else []))
        elif w in ("omA", "omB"):
            k = plan["om"].get(w[2] + str(m))
            if k is None: return True
            a = k * TK
            ts(w, T.om[:, a:a + TK], T.zr[:, a:a + TK], T.icb[:, 0:1], None, [ALU.not_equal], ["zr", "icb"], [("om", a, a + TK)], ["zr", "icb"], oms(a, a + TK))
        elif w == "Lzc": dma(q, "zc", [(T.zc[:, :], T.zo[:, :])], [], ["zc"])
        elif w == "zsq": act(w, T.zc2[:, :], T.zc[:, :], AF.Square, None, ["zc"], ["zc2"], ["zc"])
        elif w == "Lzq": dma(q, "zq", [(T.zq[0:8, :], T.zc2[:, :])], ["zc2"], ["zq"], ["zsq"])
        elif w == "i2": act(w, col(2), col(0), AF.Square, None, [cr(0)], [cr(2)], ["icol"])
        elif w == "m2i": add(q, w, lambda: g.iota(T.m2i[0:8, :], [[0, 8], [-2, 16]], 0, 0, allow_small_or_imprecise_dtypes=True), [], [w], [])
        elif w == "s2i": asel(w, T.s2i[0:8, :], T.m2i[0:8, :], [[1, 8], [0, 16]], ALU.is_equal, 0, -1, ["m2i"], [w])
        elif w in ("oq0", "oq1", "ol0", "ol1"):
            k = 2 * (m + 1) + int(w[2]); b = db(m, 1 + int(w[2])); a = k * 512
            free = freed(m, 1 + int(w[2])) + oms(m * TK, m * TK + TK) if w[1] == "q" else ["cN%d_%d" % (m, 1 + int(w[2]))]
            mm("oq%d" % k, [(T[b][:, 0:512], T.s2i[0:8, :], T.zt[0:8, a:a + 512], True, False), (T[b][:, 0:512], T.sel[0:8, :], T.zq[0:8, a:a + 512], False, True)],
               ["sel", "s2i", "zt", "zq"], [b], ["sel", "s2i", "zo", "zq"] + free)
        elif w in ("os0", "os1"):
            k = 2 * (m + 1) + int(w[2]); b = db(m, 1 + int(w[2])); a = k * 512
            act("om%d" % k, T.om[:, a:a + 512], T[b][:, 0:512], AF.Sign, col(2), [b, cr(2)], [("om", a, a + 512)], ["oq%d" % k, "i2"])
        elif w == "Lcv": dma(q, "conv", [(T.doc[:, CS:D], T.nd[:, CS:D])], [], [("doc", CS, D)], ["eye"])
        elif w == "cvS": act(w, T.doc[:, 0:CS], T.ndb[:, 0:CS], AF.Silu, UP, ["ndb"], [("doc", 0, CS)], ["nd"])
        elif w == "cvV": ts("conv", T.doc[:, CS:D], T.ndb[:, CS:D], UP, None, [ALU.add], ["ndb"], [("doc", CS, D)], ["nd"])
        elif w[:2] == "om":
            k = int(w[2:]); b = zb_bank(k)
            ts(w, T.om[:, k * 512:(k + 1) * 512], T[b][:, 0:512], col(0), None, [ALU.not_equal], [b, cr(0)], [("om", k * 512, (k + 1) * 512)], ["zb%d" % k, "icol"])
        elif w == "conv": act(w, T.doc[:, :], T.ndb[:, :], AF.Identity if plan["early"] else AF.Silu, None, ["ndb"], ["doc"], ["nd"])
        elif w[:3] == "off":
            h = int(w[3]); a = (2 * h + 1) * 64
            remote(w, T.nbo[:, h * 64:h * 64 + 64], T.wlu[:, a:a + 64], [("wlu", a, a + 64)], [("nbo", h, h + 1)], lists(2 * h + 1, "iw"), ["a_" + w])
        elif w[:3] == "blk":
            a, b = "W%d" % (m // 2), "W%d" % (m // 2 + 1)
            remote("blk" + b[1], T[b][:, :], T[a][:, :], [a], [b], last("sb", m), ["a_blk" + b[1]])
        elif w == "Syw": dma(q, "yw", [(T.yw[:, :], T.W2[:, :])], ["W2"], [], last("sb"))
        elif w[:3] == "fin":
            a = int(w[3]) * TK
            if q == "v": ts(w, T.ydb[:, a:a + TK], T.doc[:, a:a + TK], MAGIC - UP, MAGIC, [ALU.add, ALU.subtract], ["doc"], [("ydb", a, a + TK)], last("sa"))
            else: act(w, T.ydb[:, a:a + TK], T.doc[:, a:a + TK], AF.Relu, -UP - 2.0 ** -10, ["doc"], [("ydb", a, a + TK)], last("sa"))
        elif w[:2] in ("fq", "fs", "fv"):
            a = int(w[2]) * 512; y = T.ydb[:, a:a + 512]; r = [("ydb", a, a + 512)]
            if w[1] == "q": ts(w, y, T.doc[:, a:a + 512], MAGIC, MAGIC, [ALU.add, ALU.subtract], ["doc"], r, last("sa"))
            elif w[1] == "s": act(w, y, T.doc[:, a:a + 512], AF.Identity, OFF, ["doc"], r, last("sa"))
            else: ts(w, y, y, -OFF, None, [ALU.add], r, r, ["fs" + w[2]], ["fq" + w[2]])
        elif w[:3] == "Syd":
            a = int(w[3]) * TK
            dma(q, w[1:], [(T.yd[:, a:a + TK], T.ydb[:, a:a + TK])], [("ydb", a, a + TK)], [],
                ["fin" + w[3]] if "fin0" in plan["last"]["v"] else ["fq%d" % (a // 512), "fq%d" % (a // 512 + 1)])
        elif w == "zcp": plus(q, w, T.zs[0:96, :], T.ZZ[0:96, 0:512], 120.0, ["ZZ"], ["zs"], ["Z5_1"])
        elif w == "Syz": dma(q, "yz", [(T.yz[:, :], T.zs[0:96, :])], ["zs"], [], ["zcp"])
        else: return False
        return True

    def chunk(q, m, w):
        k = w.rstrip("0123456789")
        cs = [int(x) for x in w[len(k):]]
        if k == "XO": m = 0 if m == "start" else m + 1
        h = m // 2
        CH = plan.get("ch" + KIND[m], plan["ch"])
        tag = lambda kk, cc=None, mb=m: ["%s%d_%d" % (kk, mb, c) for c in (cs if cc is None else cc)]
        c0 = cs[0]; a, b = CH[c0], CH[cs[-1] + 1]; u = b - a
        t0, t1 = m * TK + a, m * TK + b
        o0, o1 = t0 // 16, t1 // 16
        e0, e1 = h * TK + a, h * TK + b
        s0, s1 = (m % 2) * TK + a, (m % 2) * TK + b
        p0 = a + c0 * PAD
        X = "P%d" % c0; Dk = db(m, c0); Wk = "W%d" % h
        nhi = KIND[m] in plan["nhi"]
        N, n0 = (X, 256) if nhi else (Dk, 0)
        name = "%s_%d" % (w, m)
        me = tag(k)
        blocks = range(0, u, B)
        wordw = lambda: T[Wk][:, 0:W].indirect(T.wlu[:, o0:o1])
        if k == "gx":
            src, prev, bias = ("ndb", ["nd"], OFF) if m == 0 else ("doc", last("sa", m - 1), OFF - UP)
            act(name, T.ag[:, a:b], T[src][:, 0:D].indirect(T.dlu[:, o0:o1]), AF.Identity, bias, [src, ("dlu", o0, o1)], [("ag", a, b)], prev + lists(m, "id"), me)
        elif k == "gy":
            prev = ["nw"] if m == 0 else last("sb", m - 1)
            tt(name, T.y1[:, t0:t1], wordw(), T.om[:, t0:t1], ALU.add, [Wk, ("wlu", o0, o1), ("om", t0, t1)], [("y1", t0, t1)], prev + oms(t0, t1) + lists(m, "iw"), me)
        elif k == "XO":
            mm(name, [(T[X][:, 0:u], T.lx[:, :], T.om[:, t0:t1], True, False)], ["lx", ("om", t0, t1)], [X], ["lx"] + oms(t0, t1) + (tag("cA", None, m - 1) if m else []), me)
        elif k == "Xa": mm(name, [(T[X][:, 0:u], T.eye[:, :], T.ag[:, a:b], False, True)], ["eye", ("ag", a, b)], [X], tag("XO") + tag("gx"), me)
        elif k == "w": tt(name, T.wp[:, a:b], T[X][:, 0:u], T.y1[:, t0:t1], ALU.mult, [X, ("y1", t0, t1)], [("wp", a, b)], tag("Xa") + tag("gy"), me)
        elif k == "Dt":
            prev = freed(m, c0) + (["om%d" % (2 * m + 1 + c0)] if c0 in (1, 2) and "oq0" in plan[KIND[m]]["t"] else [])
            mm(name, [(T[Dk][:, j:j + B], T.wp[:, a + j:a + j + B], T.rw[:, h * B:(h + 1) * B], True, True) for j in blocks],
               [("rw", h, h + 1), ("wp", a, b)], [Dk], tag("w") + prev + ["rw%d" % h], me)
        elif k == "sc":
            add(q, name, lambda: V.tensor_tensor_scan(T.ee[:, a:b], T.vp[:, s0:s1], T[Dk][:, 0:u], 0.0, ALU.mult, ALU.add),
                [Dk, ("vp", s0, s1)], [("ee", a, b)], tag("Dt") + ["vf%d" % m], me)
        elif k == "vc": ts(name, T.cv[:, p0:p0 + u], T.ee[:, a:b], 0.0, 2.0, [ALU.is_ge, ALU.mult], [("ee", a, b)], [("cv", p0, p0 + u)], tag("sc") + ["padv"], tag("cm"))
        elif k == "cm": act(name, T.cs[:, p0:p0 + u], T.ee[:, a:b], AF.Sign, 0.5, [("ee", a, b)], [("cs", p0, p0 + u)], tag("sc") + ["pads"], me)
        elif k == "bk":
            c = "cv" if ("vc%d" % c0) in plan[KIND[m]]["v"].split() else "cs"
            mm(name, [(T[N][:, n0 + j:n0 + j + B], T[c][:, p0 + j + i:p0 + j + i + B], T[("hp", "hn")[i]][:, :], i == 0, i == 1) for j in blocks for i in (0, 1)],
               ["hp", "hn", (c, p0, p0 + u + PAD)], [N], tag("cm") + ["hp", "hn"], me)
        elif k == "cN":
            if q == "s":
                add(q, name, lambda: S.activation(T.nm[:, t0:t1], T[N][:, n0:n0 + u], AF.Identity, bias=col(1), scale=1.0 / 64),
                    [N, cr(1)], [("nm", t0, t1)], tag("bk") + ["e15"], me)
            else: ts(name, T.nm[:, t0:t1], T[N][:, n0:n0 + u], 1.0 / 64, col(1), [ALU.mult, ALU.add], [N, cr(1)], [("nm", t0, t1)], tag("bk") + ["e15"], me)
        elif k == "Np":
            mm(name, [(T[X][:, 0:u], T.lx[:, :], T.om[:, t0:t1], True, False), (T[X][:, 0:u], T.eye[:, :], T.ag[:, a:b], False, False)],
               ["lx", "eye", ("om", t0, t1), ("ag", a, b)], [X], tag("cN" if nhi else "w"), me)
        elif k == "NA": mm(name, [(T[X][:, 0:u], T.eye[:, :], T.nm[:, t0:t1], False, True)], ["eye", ("nm", t0, t1)], [X], tag("cN") + tag("Np"), me)
        elif k == "bA":
            c = "cv" if ("vc%d" % c0) in plan[KIND[m]]["v"].split() else "cs"
            mm(name, [(T[X][:, j:j + B], T[c][:, p0 + j + i:p0 + j + i + B], T[("hq", "hr")[i]][:, :], False, i == 1 and j + B == u) for j in blocks for i in (0, 1)],
               ["hq", "hr", (c, p0, p0 + u + PAD)], [X], tag("cm") + tag("Np") + ["hq", "hr"], tag("NA"))
        elif k == "cA" and ("bA%d" % c0) in plan[KIND[m]]["t"].split():
            plus(q, name + "b", T.na[:, a:b], T[X][:, 0:u], col(1), [X, cr(1)], [("na", a, b)], tag("NA"), me)
        elif k == "cA": plus(q, name, T.na[:, a:b], T[X][:, 0:u], UP, [X], [("na", a, b)], tag("NA"), me)
        elif k == "vA": tt(name, T.na[:, a:b], T[X][:, 0:u], T.nm[:, t0:t1], ALU.add, [X, ("nm", t0, t1)], [("na", a, b)], tag("cN"), tag("cA"))
        elif k == "sa":
            act(name, T.doc[:, 0:D].indirect(T.dlu[:, o0:o1]), T.na[:, a:b], AF.Silu, None, [("na", a, b), ("dlu", o0, o1)], ["doc"],
                tag("cA") + ["conv"] + (["cvS"] if CS else []), me)
        elif k == "sb":
            tt(name, wordw(), T.y1[:, t0:t1], T.nm[:, t0:t1], ALU.add, [("y1", t0, t1), ("nm", t0, t1), ("wlu", o0, o1)], [Wk], tag("cN"), me)
        elif k in ("sy", "sn"):
            src, land = (("y1", "yrecv"), ("nm", "nrecv"))[k == "sn"]
            remote("%s%d_%d" % (k[1], h, c0), T[land][:, e0:e1], T[src][:, t0:t1], [(src, t0, t1)], [(land, e0, e1)], tag("gy" if k == "sy" else "cN"), tag("a" + k))
        elif k == "sf":
            both((T.yrecv[:, e0:e1], T.nrecv[:, e0:e1]), (T.y1[:, t0:t1], T.nm[:, t0:t1]), "n%d_%d" % (h, c0), [("y1", t0, t1), ("nm", t0, t1)],
                 [("yrecv", e0, e1), ("nrecv", e0, e1)], tag("cN"), tag("asy") + tag("asn"))
        elif k == "nb": tt(name, T.nsend[:, e0:e1], T[N][:, n0:n0 + u], T.y1[:, t0:t1], ALU.add, [N, ("y1", t0, t1)], [("nsend", e0, e1)], tag("bk"), me)
        elif k == "sd": remote("n%d_%d" % (h, c0), T.nrecv[:, e0:e1], T.nsend[:, e0:e1], [("nsend", e0, e1)], [("nrecv", e0, e1)], tag("nb"), tag("asn"))
        elif k == "rs" and sums:
            Wn = "W%d" % (h + 1)
            tt(name, T[Wn][:, 0:W].indirect(T.nbo[:, h * 64 + a // 16:h * 64 + b // 16]), T.nrecv[:, e0:e1], T.kc[:, 0:u], ALU.add,
               [("nrecv", e0, e1), "kc", ("nbo", h, h + 1)], [Wn], tag("asn") + ["kc", "a_off%d" % h, "a_blk%d" % (h + 1)], tag("sb"))
        elif k == "rs":
            Wn = "W%d" % (h + 1)
            tt(name, T[Wn][:, 0:W].indirect(T.nbo[:, h * 64 + a // 16:h * 64 + b // 16]), T.yrecv[:, e0:e1], T.nrecv[:, e0:e1], ALU.add,
               [("yrecv", e0, e1), ("nrecv", e0, e1), ("nbo", h, h + 1)], [Wn],
               tag("asy") + tag("asn") + ["a_off%d" % h, "a_blk%d" % (h + 1)], tag("sb"))
        elif k == "Z":
            j = 2 * m + c0
            z0 = m * TK + c0 * 512
            mm(name, [(T.ZZ[0:96, 0:512], T.zw[:, 11 - j:107 - j], T.nm[:, z0:z0 + 512], j == 0, j == 11)], ["zw", ("nm", z0, z0 + 512)], ["ZZ"],
               tag("cN", [c for c in range(NC) if CH[c] < c0 * 512 + 512 and CH[c + 1] > c0 * 512]) + ["zw1", "vT"] + (["Z%d_%d" % divmod(j - 1, 2)] if j else []), me)
        else: raise ValueError(w)

    for m in ["start"] + list(range(M)):
        for q in "ysvtg":
            for w in plan[m if m == "start" else KIND[m]].get(q, "").split():
                if m in ("start", ONLY.get(w, m)) and not fixed(q, w, m): chunk(q, m, w)

    order, have, pos = [], set(), {q: 0 for q in queues}
    moved = True
    while moved:
        moved = False
        for q in queues:
            while pos[q] < len(queues[q]) and all(x in have for x in queues[q][pos[q]]["needs"]):
                o = queues[q][pos[q]]; order.append(o); have.update(o["gives"]); pos[q] += 1; moved = True
    stuck = [(q, queues[q][pos[q]]["name"], [x for x in queues[q][pos[q]]["needs"] if x not in have]) for q in queues if pos[q] < len(queues[q])]
    if stuck:
        raise ValueError("order: %r" % (stuck,))
    return order, neng, nin


def emit(order, neng, nin, g, T):
    eng = {"y": g.sync, "s": g.scalar, "g": g, "v": g.vector, "t": g.tensor}
    count = {k: 0 for k in "vstg"}
    known = {q: {} for q in eng}
    hist, ends, sent = {}, {}, 0
    for o in order:
        q = o["q"]
        deps = []
        for write, regs in ((False, o["R"]), (True, o["W"])):
            for (b, lo, hi) in regs:
                for e in hist.get(b, []):
                    if b in BANKS:
                        if e[3]["q"] != q: deps.append(e[3])
                    elif e[0] < hi and lo < e[1] and (write or e[2]):
                        deps.append(e[3])
        if o["kind"] != "a":
            kn = known[q]
            need = {}
            for d in deps:
                s, v = d["sig"]
                if kn.get(s, 0) < v: need[s] = max(need.get(s, 0), v)
            for d in deps:
                for s, v in d["clock"].items():
                    if s != d["sig"][0] and s in need and need[s] <= v:
                        del need[s]
            for s in sorted(need):
                eng[q].wait_ge(T.sem[s], need[s])
            for d in deps:
                for s, v in d["clock"].items():
                    if kn.get(s, 0) < v: kn[s] = v
            ins = o["fn"]()
            if o["kind"] == "c":
                for i in (ins if isinstance(ins, list) else [ins]):
                    count[q] += 1
                    i.then_inc(T.sem["c" + q], 1)
                o["sig"] = ("c" + q, count[q])
            elif o["kind"] == "d":
                for i in ins:
                    i.then_inc(T.sem["d_" + o["name"]], 16)
                o["sig"] = ("d_" + o["name"], 16 * len(ins))
            else:
                sent += neng
                o["sig"] = ("sent", sent)
            o["clock"] = dict(kn)
        else:
            o["sig"] = ("a_" + o["name"], nin)
            o["clock"] = {}
        o["clock"][o["sig"][0]] = o["sig"][1]
        ends[o["sig"][0]] = o["sig"][1]
        for (b, lo, hi) in o["W"]:
            hist[b] = [e for e in hist.get(b, []) if not (lo <= e[0] and e[1] <= hi)] + [(lo, hi, True, o)]
        for (b, lo, hi) in o["R"]:
            hist.setdefault(b, []).append((lo, hi, False, o))
    for s in sorted(ends):
        g.sync.wait_ge(T.sem[s], ends[s])


def rank_program(g, core, T, topo):
    if T.rank_of(core) is None:
        return
    order, neng, nin = build(T, topo, core, g, PLAN)
    emit(order, neng, nin, g, T)
